import numpy as np
import ml_dtypes


def mxq(x, axis, fmt="e4m3"):
    dtype, down = {"e4m3": (ml_dtypes.float8_e4m3fn, 7), "e5m2": (ml_dtypes.float8_e5m2, 14)}[fmt]
    v = np.moveaxis(np.asarray(x, np.float32).astype(ml_dtypes.bfloat16).astype(np.float64), axis, -1)
    blocks = v.reshape(v.shape[:-1] + (-1, 32))
    amax = np.abs(blocks).max(-1, keepdims=True)
    byte = np.maximum(np.where(amax > 0, np.frexp(amax)[1] - 1 + 127, 0) - down, 1)
    scale = np.exp2(byte - 127.0)
    codes = (blocks / scale).astype(np.float32).astype(dtype).astype(np.float64)
    return np.moveaxis((codes * scale).reshape(v.shape), -1, axis)


WIDE = False


def mx_kscale(k):
    if not WIDE:
        return np.ones(k)
    levels = np.array([18, -18])
    if k % 512:
        return np.exp2(np.random.permutation(np.resize(levels, k // 32))).repeat(32)
    a = np.empty((k // 512, 16))
    for p in range(k // 512):
        a[p, :8] = np.random.permutation(np.resize(levels, 8))
        for g in range(8):
            far = levels[np.abs(levels - a[p, g]) >= 10]
            a[p, g + 8] = far[np.random.randint(len(far))]
    return np.exp2(a.ravel()).repeat(32)


def f64(x):
    return np.asarray(x).astype(np.float64)


def striped(idx):
    return np.tile(np.asarray(idx).reshape(-1, 16).T, (8, 1)).astype(np.uint16)


def unstriped(offs):
    return offs[:16].T.reshape(-1).astype(np.int64)

def planes(y):
    n, m = y.shape
    v = y.astype(np.float32).astype(ml_dtypes.bfloat16).astype(np.float64).reshape(n // 32, 32, m)
    top = np.abs(v).max(1)
    byte = np.clip(np.where(top > 0, np.frexp(top)[1] - 1 + 127 - 7, 1), 1, 254)
    codes = (v * np.exp2(127.0 - byte)[:, None, :]).reshape(n, m).astype(np.float32).astype(ml_dtypes.float8_e4m3fn).view(np.uint8)
    words = codes.reshape(n // 512, 128, 4, m).transpose(0, 1, 3, 2)
    return np.ascontiguousarray(words), np.ascontiguousarray(byte.astype(np.uint8).reshape(n // 512, 16, m))


B, N, T, D, R = 1, 512, 2048, 512, 512
LR = 0.1
WD = 0.5


def setup_inputs():
    n = np.random.standard_normal
    idx = np.random.permutation(T)[:B * N]
    s = mx_kscale(D)[:, None]
    z = mx_kscale(R)[:, None]
    x = n((B, D, R))
    return {
        "xT": (x * s).astype(np.float32),
        "wT": (n((D, T)) * (1.00 / np.sqrt(D)) / s).astype(np.float32),
        "y": n((B, R, N)).astype(np.float32),
        "wt": (np.random.uniform(0.5, 1.5, (B, R, 1)) * 1.0 / np.sqrt(R) * z).astype(np.float32),
        "xm": (x.transpose(0, 2, 1) / z / s[:, 0]).astype(np.float32),
        "offs": striped(idx),
    }


def reference(xT, wT, y, wt, xm, offs):
    idx = unstriped(offs)
    pick = lambda x: x[:, idx].reshape(x.shape[0], B, N).transpose(1, 0, 2)
    w = pick(f64(wT))
    a = mxq(f64(xT), 1, "e4m3").transpose(0, 2, 1) @ mxq(w, 1, "e4m3")
    g = f64(wt) * np.minimum(np.maximum(a - f64(y), -1.0), 1.0)
    dw = mxq(f64(xm), 1, "e4m3").transpose(0, 2, 1) @ mxq(g, 1, "e5m2")
    nw = (1.0 - LR * WD) * w - LR * dw
    tables = []
    for old, new in ((wT, nw),):
        table = f64(old)
        table[:, idx] = new.transpose(1, 0, 2).reshape(D, B * N)
        tables.append(table)
    return tuple(tables) + planes(tables[0])

@@ -1,0 +1,268 @@
+from contextlib import ExitStack
+
+import concourse.mybir as mybir
+
+D, T, N, R = 512, 2048, 512, 512
+LR, WD = 0.1, 0.5
+FLOPS = 2 * 2 * R * D * N
+
+F32 = mybir.dt.float32
+BF16 = mybir.dt.bfloat16
+I32 = mybir.dt.int32
+U32 = mybir.dt.uint32
+U16 = mybir.dt.uint16
+U8 = mybir.dt.uint8
+E4M3 = mybir.dt.float8_e4m3fn_x4
+E5M2 = mybir.dt.float8_e5m2_x4
+ALU = mybir.AluOpType
+COPY = mybir.ActivationFunctionType.Copy
+
+P = 128
+LANES = 4
+HALF = 64
+H = N // 2
+CHUNKS = [(0, 256), (256, 768), (768, 1280), (1280, 1536), (1536, 1792), (1792, 2048)]
+SCALAR_WEAVES = 2
+
+
+def deal_copy(copy, dealt, raw, first, lo, hi):
+    copy(
+        out=dealt[:, :, lo:hi, :].rearrange("p t s j -> p s j t"),
+        in_=raw[:, :, LANES * (lo - first) : LANES * (hi - first)].rearrange("p j (s t) -> p s j t", t=LANES),
+    )
+
+
+def weave_words(copy, woven, pairs):
+    copy(
+        out=woven[:].rearrange("p c l -> p (c l)").bitcast(F32).rearrange("p (c h) -> p c h", h=2),
+        in_=pairs[:].rearrange("p h c e -> p h (c e)").bitcast(F32).rearrange("p h c -> p c h"),
+    )
+
+
+def tile_attend_ghub_pl_sgd_kernel(tc, xT, wT, y, wt, xm, offs, out_0, out_1, out_2):
+    nc = tc.nc
+    w_rows = wT.rearrange("(p t) c -> p t c", t=LANES)
+    out_rows = out_0.rearrange("(p t) c -> p t c", t=LANES)
+    x_rows = xT[0].rearrange("(p j) r -> p j r", j=LANES)
+    xm_rows = xm[0].rearrange("(p j) d -> p j d", j=LANES)
+    y_rows = y[0].rearrange("(p t) i -> p t i", t=LANES)
+    wt_rows = wt[0].rearrange("(p t) o -> p (t o)", t=LANES)
+    words_out = out_1[0].rearrange("p c l -> p (c l)").bitcast(I32)
+    scales_out = out_2[0].bitcast(I32)
+
+    with ExitStack() as ctx:
+        pool = ctx.enter_context(tc.tile_pool(name="pool", bufs=1))
+        psum = ctx.enter_context(tc.psum_pool(name="psum", bufs=1))
+
+        offsets = pool.tile([P, N // 16], U16, name="offsets")
+        source = [pool.tile([P, T], F32, name="source%d" % t) for t in range(LANES)]
+        table = [pool.tile([P, T], F32, name="table%d" % t) for t in range(LANES)]
+        x_raw = pool.tile([P, LANES, R], F32, name="x_raw")
+        xm_raw = [pool.tile([P, LANES, D // 2], F32, name="xm_raw%d" % h) for h in range(2)]
+        y_raw = [pool.tile([P, N], F32, name="y_raw%d" % t) for t in range(LANES)]
+        weight = pool.tile([P, LANES], F32, name="weight")
+
+        nc.sync.dma_start(out=x_raw[:], in_=x_rows)
+        nc.sync.dma_start(offsets[:], offs)
+        nc.scalar.dma_start(out=weight[:], in_=wt_rows)
+        for t in range(LANES):
+            nc.sync.dma_start(out=source[t][:], in_=w_rows[:, t, :])
+        for t in range(LANES):
+            nc.sync.dma_start(out=y_raw[t][:], in_=y_rows[:, t, :])
+        for h in range(2):
+            nc.sync.dma_start(out=xm_raw[h][:], in_=xm_rows[:, :, h * D // 2 : (h + 1) * D // 2])
+        for t in range(LANES):
+            nc.sync.dma_start(out=table[t][:], in_=w_rows[:, t, :])
+
+        upper = pool.tile([P, LANES], F32, name="upper")
+        lower = pool.tile([P, LANES], F32, name="lower")
+        nc.vector.scalar_tensor_tensor(upper[:], weight[:], -1.0, weight[:], ALU.mult, ALU.max)
+        nc.vector.scalar_tensor_tensor(lower[:], weight[:], -1.0, weight[:], ALU.mult, ALU.min)
+
+        g_codes = pool.tile([P, N], U32, name="g_codes", align_bytes=64)
+        g_scales = pool.tile([P, N], U8, name="g_scales", align_bytes=64)
+        nc.vector.memset(g_codes[:, H:N], 0)
+        nc.vector.memset(g_scales[:, H:N].bitcast(U32), 0)
+
+        x16 = pool.tile([P, LANES, P, LANES], BF16, name="x16", align_bytes=64)
+        deal_copy(nc.vector.tensor_copy, x16, x_raw, 0, 0, P)
+        x_codes = [pool.tile([P, P], U32, name="x_codes%d" % t, align_bytes=64) for t in range(LANES)]
+        x_scales = [pool.tile([P, P], U8, name="x_scales%d" % t, align_bytes=64) for t in range(LANES)]
+        for t in range(LANES):
+            nc.vector.quantize_mx(
+                out=x_codes[t][:].bitcast(E4M3),
+                scales=x_scales[t][:],
+                in_=x16[:, t, :, :].rearrange("p s j -> p (s j)"),
+            )
+
+        halves = [slice(0, H), slice(H, N)]
+        picked = [pool.tile([P, N], F32, name="picked%d" % t) for t in range(LANES)]
+        w16 = [pool.tile([P, H, LANES], BF16, name="w16_%d" % h, align_bytes=64) for h in range(2)]
+        decayed = []
+        for t in range(LANES):
+            if t < LANES - 1:
+                nc.vector.tensor_copy(picked[t][:], source[t][:].indirect(offsets[:]))
+            else:
+                for h in range(2):
+                    listed = offsets[:, h * H // 16 : (h + 1) * H // 16]
+                    nc.vector.tensor_copy(picked[t][:, halves[h]], source[t][:].indirect(listed))
+            nc.scalar.copy(out=w16[0][:, :, t], in_=picked[t][:, halves[0]])
+            nc.vector.tensor_copy(out=w16[1][:, :, t], in_=picked[t][:, halves[1]])
+        for t in range(LANES - 1):
+            kept = pool.tile([P, N], F32, name="decayed%d" % t)
+            nc.scalar.activation(kept[:], picked[t][:], COPY, scale=1.0 - LR * WD)
+            decayed.append(kept)
+
+        scores = []
+        for h in range(2):
+            w_codes = pool.tile([P, H], U32, name="w_codes%d" % h, align_bytes=64)
+            w_scales = pool.tile([P, H], U8, name="w_scales%d" % h, align_bytes=64)
+            nc.vector.quantize_mx(
+                out=w_codes[:].bitcast(E4M3), scales=w_scales[:], in_=w16[h][:].rearrange("p i t -> p (i t)")
+            )
+            banks = [psum.tile([P, 2, H], F32, name="scores%d_%d" % (h, u)) for u in range(2)]
+            for t in range(LANES):
+                nc.tensor.matmul_mx(
+                    out=banks[t // 2][:, t % 2, :],
+                    lhsT=x_codes[t][:].bitcast(E4M3),
+                    lhsT_scale=x_scales[t][:],
+                    rhs=w_codes[:].bitcast(E4M3),
+                    rhs_scale=w_scales[:],
+                    start=True,
+                    stop=True,
+                )
+            scores.append(banks)
+
+        weighted_y = [pool.tile([P, N], F32, name="weighted_y%d" % t) for t in range(LANES)]
+        for h in range(2):
+            for t in range(LANES):
+                nc.scalar.activation(
+                    weighted_y[t][:, halves[h]], y_raw[t][:, halves[h]], COPY, scale=weight[:, t : t + 1]
+                )
+
+        xm16 = pool.tile([P, LANES, P, LANES], BF16, name="xm16", align_bytes=64)
+        for h in range(2):
+            deal_copy(nc.scalar.copy, xm16, xm_raw[h], h * HALF, h * HALF, (h + 1) * HALF)
+        kept = pool.tile([P, N], F32, name="xm_raw1")
+        nc.scalar.activation(kept[:], picked[LANES - 1][:], COPY, scale=1.0 - LR * WD)
+        decayed.append(kept)
+
+        g_pairs = [pool.tile([P, 2, H, 2], BF16, name="g_pairs%d" % h) for h in range(2)]
+        g16 = [pool.tile([P, H, LANES], BF16, name="g16_%d" % h, align_bytes=64) for h in range(2)]
+        residual = [pool.tile([P, N], F32, name="residual%d" % t) for t in range(LANES)]
+        xm_codes = [pool.tile([P, P], U32, name="xm_codes%d" % t, align_bytes=64) for t in range(LANES)]
+        xm_scales = [pool.tile([P, P], U8, name="xm_scales%d" % t, align_bytes=64) for t in range(LANES)]
+
+        def subtract_targets(h, t):
+            nc.vector.scalar_tensor_tensor(
+                residual[t][:, halves[h]],
+                scores[h][t // 2][:, t % 2, :],
+                weight[:, t : t + 1],
+                weighted_y[t][:, halves[h]],
+                ALU.mult,
+                ALU.subtract,
+            )
+
+        def clamp(h, t):
+            nc.vector.tensor_scalar(
+                g_pairs[h][:, t // 2, :, t % 2],
+                residual[t][:, halves[h]],
+                lower[:, t : t + 1],
+                upper[:, t : t + 1],
+                ALU.max,
+                ALU.min,
+            )
+
+        def quantize_g(h):
+            nc.vector.quantize_mx(
+                out=g_codes[:, halves[h]].bitcast(E5M2),
+                scales=g_scales[:, halves[h]],
+                in_=g16[h][:].rearrange("p i t -> p (i t)"),
+            )
+
+        def quantize_xm(t):
+            nc.vector.quantize_mx(
+                out=xm_codes[t][:].bitcast(E4M3),
+                scales=xm_scales[t][:],
+                in_=xm16[:, t, :, :].rearrange("p s j -> p (s j)"),
+            )
+
+        def gradient(t, name):
+            bank = psum.tile([P, N], F32, name=name)
+            nc.tensor.matmul_mx(
+                out=bank[:],
+                lhsT=xm_codes[t][:].bitcast(E4M3),
+                lhsT_scale=xm_scales[t][:],
+                rhs=g_codes[:].bitcast(E5M2),
+                rhs_scale=g_scales[:],
+                start=True,
+                stop=True,
+            )
+            return bank
+
+        subtract_targets(0, 0)
+        for t in range(1, LANES):
+            subtract_targets(0, t)
+            clamp(0, t - 1)
+        subtract_targets(1, 0)
+        clamp(0, LANES - 1)
+        subtract_targets(1, 1)
+        weave_words(nc.vector.tensor_copy, g16[0], g_pairs[0])
+        clamp(1, 0)
+        subtract_targets(1, 2)
+        quantize_g(0)
+        clamp(1, 1)
+        subtract_targets(1, 3)
+        clamp(1, 2)
+        quantize_xm(0)
+        early_bank = gradient(0, "scores0_0")
+        clamp(1, 3)
+        quantize_xm(1)
+        weave_words(nc.vector.tensor_copy, g16[1], g_pairs[1])
+        early_step = pool.tile([P, H], F32, name="g_pairs1")
+        nc.scalar.activation(early_step[:], early_bank[:, halves[0]], COPY, scale=-LR)
+        quantize_xm(2)
+        quantize_g(1)
+        quantize_xm(3)
+
+        steps = []
+        for t in range(LANES):
+            bank = gradient(t, "gradient%d" % t)
+            slots = halves[1] if t == 0 else slice(0, N)
+            step = pool.tile([P, slots.stop - slots.start], F32, name="step%d" % t)
+            nc.scalar.activation(step[:], bank[:, slots], COPY, scale=-LR)
+            steps.append(step)
+
+        pairs = [pool.tile([P, 2, hi - lo, 2], BF16, name="pairs%d" % lo) for lo, hi in CHUNKS]
+        for t in range(LANES):
+            if t == 0:
+                for h, step in enumerate([early_step, steps[0]]):
+                    listed = offsets[:, h * H // 16 : (h + 1) * H // 16]
+                    nc.vector.tensor_tensor(table[t][:].indirect(listed), decayed[t][:, halves[h]], step[:], ALU.add)
+            else:
+                nc.vector.tensor_tensor(table[t][:].indirect(offsets[:]), decayed[t][:], steps[t][:], ALU.add)
+            nc.sync.dma_start(out=out_rows[:, t, :], in_=table[t][:])
+            for c, (lo, hi) in enumerate(CHUNKS):
+                copy = nc.vector.tensor_copy if c == 0 and t >= 2 else nc.scalar.copy
+                copy(out=pairs[c][:, t // 2, :, t % 2], in_=table[t][:, lo:hi])
+
+        out_scales = pool.tile([P, T], U8, name="out_scales", align_bytes=64)
+        woven = [pool.tile([P, hi - lo, LANES], BF16, name="woven%d" % lo, align_bytes=64) for lo, hi in CHUNKS]
+        last = len(CHUNKS) - 1
+
+        def quantize_out(c):
+            lo, hi = CHUNKS[c]
+            codes = pool.tile([P, hi - lo], U32, name="out_codes%d" % c, align_bytes=64)
+            nc.vector.quantize_mx(
+                out=codes[:].bitcast(E4M3), scales=out_scales[:, lo:hi], in_=woven[c][:].rearrange("p c l -> p (c l)")
+            )
+            nc.sync.dma_start(out=words_out[:, lo:hi], in_=codes[:].bitcast(I32))
+
+        for c in range(len(CHUNKS)):
+            weave_words(nc.scalar.copy if c > last - SCALAR_WEAVES else nc.vector.tensor_copy, woven[c], pairs[c])
+            if c > 0:
+                quantize_out(c - 1)
+        quantize_out(last)
+        for q in range(4):
+            queue = nc.scalar if q % 2 else nc.sync
+            queue.dma_start(out=scales_out[4 * q : 4 * q + 4, :], in_=out_scales[32 * q : 32 * q + 4, :].bitcast(I32))

@@ -21,8 +21,10 @@ P = 128
 LANES = 4
 HALF = 64
 H = N // 2
-CHUNKS = [(0, 256), (256, 768), (768, 1280), (1280, 1536), (1536, 1792), (1792, 2048)]
-SCALAR_WEAVES = 2
+PASS = 512
+ORDER = [0, 2, 3, 1]
+SCALAR_CHUNKS = [(1024, 1536), (1536, 1792), (1792, 2048)]
+LATE = 16
 
 
 def deal_copy(copy, dealt, raw, first, lo, hi):
@@ -35,7 +37,7 @@ def deal_copy(copy, dealt, raw, first, lo, hi):
 def weave_words(copy, woven, pairs):
     copy(
         out=woven[:].rearrange("p c l -> p (c l)").bitcast(F32).rearrange("p (c h) -> p c h", h=2),
-        in_=pairs[:].rearrange("p h c e -> p h (c e)").bitcast(F32).rearrange("p h c -> p c h"),
+        in_=pairs.rearrange("p h c e -> p h (c e)").bitcast(F32).rearrange("p h c -> p c h"),
     )
 
 
@@ -59,7 +61,7 @@ def tile_attend_ghub_pl_sgd_kernel(tc, xT, wT, y, wt, xm, offs, out_0, out_1, ou
         table = [pool.tile([P, T], F32, name="table%d" % t) for t in range(LANES)]
         x_raw = pool.tile([P, LANES, R], F32, name="x_raw")
         xm_raw = [pool.tile([P, LANES, D // 2], F32, name="xm_raw%d" % h) for h in range(2)]
-        y_raw = [pool.tile([P, N], F32, name="y_raw%d" % t) for t in range(LANES)]
+        y_raw = [pool.tile([P, N], F32, name="y_raw%d" % t, align_bytes=64) for t in range(LANES)]
         weight = pool.tile([P, LANES], F32, name="weight")
 
         nc.sync.dma_start(out=x_raw[:], in_=x_rows)
@@ -71,7 +73,7 @@ def tile_attend_ghub_pl_sgd_kernel(tc, xT, wT, y, wt, xm, offs, out_0, out_1, ou
             nc.sync.dma_start(out=y_raw[t][:], in_=y_rows[:, t, :])
         for h in range(2):
             nc.sync.dma_start(out=xm_raw[h][:], in_=xm_rows[:, :, h * D // 2 : (h + 1) * D // 2])
-        for t in range(LANES):
+        for t in ORDER:
             nc.sync.dma_start(out=table[t][:], in_=w_rows[:, t, :])
 
         upper = pool.tile([P, LANES], F32, name="upper")
@@ -85,7 +87,7 @@ def tile_attend_ghub_pl_sgd_kernel(tc, xT, wT, y, wt, xm, offs, out_0, out_1, ou
         nc.vector.memset(g_scales[:, H:N].bitcast(U32), 0)
 
         x16 = pool.tile([P, LANES, P, LANES], BF16, name="x16", align_bytes=64)
-        deal_copy(nc.vector.tensor_copy, x16, x_raw, 0, 0, P)
+        deal_copy(nc.scalar.copy, x16, x_raw, 0, 0, P)
         x_codes = [pool.tile([P, P], U32, name="x_codes%d" % t, align_bytes=64) for t in range(LANES)]
         x_scales = [pool.tile([P, P], U8, name="x_scales%d" % t, align_bytes=64) for t in range(LANES)]
         for t in range(LANES):
@@ -96,22 +98,24 @@ def tile_attend_ghub_pl_sgd_kernel(tc, xT, wT, y, wt, xm, offs, out_0, out_1, ou
             )
 
         halves = [slice(0, H), slice(H, N)]
-        picked = [pool.tile([P, N], F32, name="picked%d" % t) for t in range(LANES)]
         w16 = [pool.tile([P, H, LANES], BF16, name="w16_%d" % h, align_bytes=64) for h in range(2)]
-        decayed = []
-        for t in range(LANES):
-            if t < LANES - 1:
-                nc.vector.tensor_copy(picked[t][:], source[t][:].indirect(offsets[:]))
-            else:
-                for h in range(2):
-                    listed = offsets[:, h * H // 16 : (h + 1) * H // 16]
-                    nc.vector.tensor_copy(picked[t][:, halves[h]], source[t][:].indirect(listed))
-            nc.scalar.copy(out=w16[0][:, :, t], in_=picked[t][:, halves[0]])
-            nc.vector.tensor_copy(out=w16[1][:, :, t], in_=picked[t][:, halves[1]])
+        decayed = [pool.tile([P, N], F32, name="decayed%d" % t) for t in range(LANES)]
+        keep = 1.0 - LR * WD
         for t in range(LANES - 1):
-            kept = pool.tile([P, N], F32, name="decayed%d" % t)
-            nc.scalar.activation(kept[:], picked[t][:], COPY, scale=1.0 - LR * WD)
-            decayed.append(kept)
+            picked = pool.tile([P, N], F32, name="picked%d" % (t % 2))
+            nc.vector.tensor_copy(picked[:], source[t][:].indirect(offsets[:]))
+            nc.scalar.copy(out=w16[0][:, :, t], in_=picked[:, halves[0]])
+            copy = nc.scalar.copy if t < 2 else nc.vector.tensor_copy
+            copy(out=w16[1][:, :, t], in_=picked[:, halves[1]])
+            nc.vector.tensor_scalar(decayed[t][:], picked[:], keep, None, ALU.mult)
+        t = LANES - 1
+        picked_halves = [pool.tile([P, H], F32, name="picked%d" % (1 - h)) for h in range(2)]
+        for h in range(2):
+            listed = offsets[:, h * H // 16 : (h + 1) * H // 16]
+            nc.vector.tensor_copy(picked_halves[h][:], source[t][:].indirect(listed))
+        nc.scalar.copy(out=w16[0][:, :, t], in_=picked_halves[0][:])
+        nc.vector.tensor_scalar(decayed[t][:, halves[0]], picked_halves[0][:], keep, None, ALU.mult)
+        nc.vector.tensor_copy(out=w16[1][:, :, t], in_=picked_halves[1][:])
 
         scores = []
         for h in range(2):
@@ -133,19 +137,16 @@ def tile_attend_ghub_pl_sgd_kernel(tc, xT, wT, y, wt, xm, offs, out_0, out_1, ou
                 )
             scores.append(banks)
 
-        weighted_y = [pool.tile([P, N], F32, name="weighted_y%d" % t) for t in range(LANES)]
+        nc.vector.tensor_scalar(decayed[LANES - 1][:, halves[1]], picked_halves[1][:], keep, None, ALU.mult)
+
+        weighted_y = [pool.tile([P, LANES, H], F32, name="picked%d" % (1 - h)) for h in range(2)]
         for h in range(2):
             for t in range(LANES):
-                nc.scalar.activation(
-                    weighted_y[t][:, halves[h]], y_raw[t][:, halves[h]], COPY, scale=weight[:, t : t + 1]
-                )
+                nc.scalar.activation(weighted_y[h][:, t, :], y_raw[t][:, halves[h]], COPY, scale=weight[:, t : t + 1])
 
-        xm16 = pool.tile([P, LANES, P, LANES], BF16, name="xm16", align_bytes=64)
+        xm16 = pool.tile([P, LANES, P, LANES], BF16, name="y_raw3", align_bytes=64)
         for h in range(2):
             deal_copy(nc.scalar.copy, xm16, xm_raw[h], h * HALF, h * HALF, (h + 1) * HALF)
-        kept = pool.tile([P, N], F32, name="xm_raw1")
-        nc.scalar.activation(kept[:], picked[LANES - 1][:], COPY, scale=1.0 - LR * WD)
-        decayed.append(kept)
 
         g_pairs = [pool.tile([P, 2, H, 2], BF16, name="g_pairs%d" % h) for h in range(2)]
         g16 = [pool.tile([P, H, LANES], BF16, name="g16_%d" % h, align_bytes=64) for h in range(2)]
@@ -158,7 +159,7 @@ def tile_attend_ghub_pl_sgd_kernel(tc, xT, wT, y, wt, xm, offs, out_0, out_1, ou
                 residual[t][:, halves[h]],
                 scores[h][t // 2][:, t % 2, :],
                 weight[:, t : t + 1],
-                weighted_y[t][:, halves[h]],
+                weighted_y[h][:, t, :],
                 ALU.mult,
                 ALU.subtract,
             )
@@ -207,62 +208,91 @@ def tile_attend_ghub_pl_sgd_kernel(tc, xT, wT, y, wt, xm, offs, out_0, out_1, ou
         subtract_targets(1, 0)
         clamp(0, LANES - 1)
         subtract_targets(1, 1)
-        weave_words(nc.vector.tensor_copy, g16[0], g_pairs[0])
+        weave_words(nc.vector.tensor_copy, g16[0], g_pairs[0][:])
         clamp(1, 0)
         subtract_targets(1, 2)
         quantize_g(0)
         clamp(1, 1)
         subtract_targets(1, 3)
         clamp(1, 2)
-        quantize_xm(0)
-        early_bank = gradient(0, "scores0_0")
+        quantize_xm(ORDER[0])
+        early_bank = gradient(ORDER[0], "scores0_0")
         clamp(1, 3)
-        quantize_xm(1)
-        weave_words(nc.vector.tensor_copy, g16[1], g_pairs[1])
+        quantize_xm(ORDER[1])
+        weave_words(nc.vector.tensor_copy, g16[1], g_pairs[1][:])
         early_step = pool.tile([P, H], F32, name="g_pairs1")
         nc.scalar.activation(early_step[:], early_bank[:, halves[0]], COPY, scale=-LR)
-        quantize_xm(2)
+        quantize_xm(ORDER[2])
         quantize_g(1)
-        quantize_xm(3)
+        quantize_xm(ORDER[3])
 
-        steps = []
-        for t in range(LANES):
-            bank = gradient(t, "gradient%d" % t)
-            slots = halves[1] if t == 0 else slice(0, N)
-            step = pool.tile([P, slots.stop - slots.start], F32, name="step%d" % t)
-            nc.scalar.activation(step[:], bank[:, slots], COPY, scale=-LR)
-            steps.append(step)
+        banks = {}
+        steps = {}
+        for t in ORDER:
+            banks[t] = gradient(t, "gradient%d" % t)
+            steps[t] = pool.tile([P, N], F32, name="step%d" % t)
+            first = H if t == ORDER[0] else 0
+            stop = N - LATE if t == ORDER[-1] else N
+            nc.scalar.activation(steps[t][:, first:stop], banks[t][:, first:stop], COPY, scale=-LR)
 
-        pairs = [pool.tile([P, 2, hi - lo, 2], BF16, name="pairs%d" % lo) for lo, hi in CHUNKS]
-        for t in range(LANES):
-            if t == 0:
-                for h, step in enumerate([early_step, steps[0]]):
+        vector_pairs = pool.tile([P, 2, 2, PASS, 2], BF16, name="vector_pairs")
+        scalar_pairs = [pool.tile([P, 2, hi - lo, 2], BF16, name="pairs%d" % lo) for lo, hi in SCALAR_CHUNKS]
+        chunks = [(0, PASS), (PASS, 2 * PASS)] + SCALAR_CHUNKS
+        pairs = [vector_pairs[:, 0], vector_pairs[:, 1]] + [tile[:] for tile in scalar_pairs]
+        woven = [pool.tile([P, hi - lo, LANES], BF16, name="woven%d" % lo, align_bytes=64) for lo, hi in chunks]
+
+        def round_chunk(copy, t, c):
+            lo, hi = chunks[c]
+            copy(out=pairs[c][:, t // 2, :, t % 2], in_=table[t][:, lo:hi])
+
+        for t in ORDER:
+            if t == ORDER[0]:
+                for h, step in enumerate([early_step[:], steps[t][:, halves[1]]]):
                     listed = offsets[:, h * H // 16 : (h + 1) * H // 16]
-                    nc.vector.tensor_tensor(table[t][:].indirect(listed), decayed[t][:, halves[h]], step[:], ALU.add)
+                    nc.vector.tensor_tensor(table[t][:].indirect(listed), decayed[t][:, halves[h]], step, ALU.add)
             else:
                 nc.vector.tensor_tensor(table[t][:].indirect(offsets[:]), decayed[t][:], steps[t][:], ALU.add)
             nc.sync.dma_start(out=out_rows[:, t, :], in_=table[t][:])
-            for c, (lo, hi) in enumerate(CHUNKS):
-                copy = nc.vector.tensor_copy if c == 0 and t >= 2 else nc.scalar.copy
-                copy(out=pairs[c][:, t // 2, :, t % 2], in_=table[t][:, lo:hi])
+            if t != ORDER[-1]:
+                nc.scalar.copy(
+                    out=vector_pairs[:, :, t // 2, :, t % 2],
+                    in_=table[t][:, 0 : 2 * PASS].rearrange("p (c i) -> p c i", c=2),
+                )
+                for c in range(2, len(chunks)):
+                    round_chunk(nc.scalar.copy, t, c)
+            if t == ORDER[0]:
+                last = ORDER[-1]
+                nc.scalar.activation(steps[last][:, N - LATE : N], banks[last][:, N - LATE : N], COPY, scale=-LR)
 
-        out_scales = pool.tile([P, T], U8, name="out_scales", align_bytes=64)
-        woven = [pool.tile([P, hi - lo, LANES], BF16, name="woven%d" % lo, align_bytes=64) for lo, hi in CHUNKS]
-        last = len(CHUNKS) - 1
+        out_scales = pool.tile([P, T // 2], U8, name="out_scales", align_bytes=64)
 
         def quantize_out(c):
-            lo, hi = CHUNKS[c]
+            lo, hi = chunks[c]
             codes = pool.tile([P, hi - lo], U32, name="out_codes%d" % c, align_bytes=64)
+            group = lo // (T // 2)
             nc.vector.quantize_mx(
-                out=codes[:].bitcast(E4M3), scales=out_scales[:, lo:hi], in_=woven[c][:].rearrange("p c l -> p (c l)")
+                out=codes[:].bitcast(E4M3),
+                scales=out_scales[4 * group : P, lo - group * T // 2 : hi - group * T // 2],
+                in_=woven[c][:].rearrange("p c l -> p (c l)"),
             )
             nc.sync.dma_start(out=words_out[:, lo:hi], in_=codes[:].bitcast(I32))
 
-        for c in range(len(CHUNKS)):
-            weave_words(nc.scalar.copy if c > last - SCALAR_WEAVES else nc.vector.tensor_copy, woven[c], pairs[c])
-            if c > 0:
-                quantize_out(c - 1)
-        quantize_out(last)
+        last = ORDER[-1]
+        for c in range(2):
+            round_chunk(nc.vector.tensor_copy, last, c)
+        for c in range(2):
+            weave_words(nc.vector.tensor_copy, woven[c], pairs[c])
+        round_chunk(nc.scalar.copy, last, 2)
+        round_chunk(nc.scalar.copy, last, 3)
+        weave_words(nc.scalar.copy, woven[2], pairs[2])
+        round_chunk(nc.scalar.copy, last, 4)
+        weave_words(nc.scalar.copy, woven[3], pairs[3])
+        weave_words(nc.scalar.copy, woven[4], pairs[4])
+        for c in range(len(chunks)):
+            quantize_out(c)
         for q in range(4):
             queue = nc.scalar if q % 2 else nc.sync
-            queue.dma_start(out=scales_out[4 * q : 4 * q + 4, :], in_=out_scales[32 * q : 32 * q + 4, :].bitcast(I32))
+            queue.dma_start(
+                out=scales_out[4 * q : 4 * q + 4, :].rearrange("f (g w) -> g f w", g=2),
+                in_=out_scales[32 * q : 32 * q + 8, :].bitcast(I32),
+            )

@@ -22,22 +22,29 @@ LANES = 4
 HALF = 64
 H = N // 2
 PASS = 512
-ORDER = [0, 2, 3, 1]
-SCALAR_CHUNKS = [(1024, 1536), (1536, 1792), (1792, 2048)]
-LATE = 16
+ORDER = [0, 1, 2, 3]
+BLOCK = 256
+BLOCKS = 4
 
 
 def deal_copy(copy, dealt, raw, first, lo, hi):
     copy(
-        out=dealt[:, :, lo:hi, :].rearrange("p t s j -> p s j t"),
-        in_=raw[:, :, LANES * (lo - first) : LANES * (hi - first)].rearrange("p j (s t) -> p s j t", t=LANES),
+        out=dealt[:, :, lo:hi, :].rearrange("p (u e) s j -> p u s j e", e=2),
+        in_=raw[:, :, LANES * (lo - first) : LANES * (hi - first)].rearrange("p j (s u e) -> p u s j e", u=2, e=2),
     )
 
 
 def weave_words(copy, woven, pairs):
     copy(
-        out=woven[:].rearrange("p c l -> p (c l)").bitcast(F32).rearrange("p (c h) -> p c h", h=2),
-        in_=pairs.rearrange("p h c e -> p h (c e)").bitcast(F32).rearrange("p h c -> p c h"),
+        out=woven.rearrange("p c l -> p (c l)").bitcast(F32).rearrange("p (k c h) -> p k c h", c=BLOCK, h=2),
+        in_=pairs.rearrange("p k h c e -> p k h (c e)").bitcast(F32).rearrange("p k h c -> p k c h"),
+    )
+
+
+def weave_rows(copy, woven, rows):
+    copy(
+        out=woven.rearrange("p (k c i) t -> p k c t i", c=BLOCK // 4, i=4),
+        in_=rows.rearrange("p k t (c i) -> p k c t i", i=4),
     )
 
 
@@ -148,7 +155,7 @@ def tile_attend_ghub_pl_sgd_kernel(tc, xT, wT, y, wt, xm, offs, out_0, out_1, ou
         for h in range(2):
             deal_copy(nc.scalar.copy, xm16, xm_raw[h], h * HALF, h * HALF, (h + 1) * HALF)
 
-        g_pairs = [pool.tile([P, 2, H, 2], BF16, name="g_pairs%d" % h) for h in range(2)]
+        g_rows = [pool.tile([P, 1, LANES, H], BF16, name="g_rows%d" % h) for h in range(2)]
         g16 = [pool.tile([P, H, LANES], BF16, name="g16_%d" % h, align_bytes=64) for h in range(2)]
         residual = [pool.tile([P, N], F32, name="residual%d" % t) for t in range(LANES)]
         xm_codes = [pool.tile([P, P], U32, name="xm_codes%d" % t, align_bytes=64) for t in range(LANES)]
@@ -166,7 +173,7 @@ def tile_attend_ghub_pl_sgd_kernel(tc, xT, wT, y, wt, xm, offs, out_0, out_1, ou
 
         def clamp(h, t):
             nc.vector.tensor_scalar(
-                g_pairs[h][:, t // 2, :, t % 2],
+                g_rows[h][:, 0, t, :],
                 residual[t][:, halves[h]],
                 lower[:, t : t + 1],
                 upper[:, t : t + 1],
@@ -208,7 +215,7 @@ def tile_attend_ghub_pl_sgd_kernel(tc, xT, wT, y, wt, xm, offs, out_0, out_1, ou
         subtract_targets(1, 0)
         clamp(0, LANES - 1)
         subtract_targets(1, 1)
-        weave_words(nc.vector.tensor_copy, g16[0], g_pairs[0][:])
+        weave_rows(nc.vector.tensor_copy, g16[0][:], g_rows[0][:])
         clamp(1, 0)
         subtract_targets(1, 2)
         quantize_g(0)
@@ -219,8 +226,8 @@ def tile_attend_ghub_pl_sgd_kernel(tc, xT, wT, y, wt, xm, offs, out_0, out_1, ou
         early_bank = gradient(ORDER[0], "scores0_0")
         clamp(1, 3)
         quantize_xm(ORDER[1])
-        weave_words(nc.vector.tensor_copy, g16[1], g_pairs[1][:])
-        early_step = pool.tile([P, H], F32, name="g_pairs1")
+        weave_rows(nc.vector.tensor_copy, g16[1][:], g_rows[1][:])
+        early_step = pool.tile([P, H], F32, name="g_rows1")
         nc.scalar.activation(early_step[:], early_bank[:, halves[0]], COPY, scale=-LR)
         quantize_xm(ORDER[2])
         quantize_g(1)
@@ -232,18 +239,22 @@ def tile_attend_ghub_pl_sgd_kernel(tc, xT, wT, y, wt, xm, offs, out_0, out_1, ou
             banks[t] = gradient(t, "gradient%d" % t)
             steps[t] = pool.tile([P, N], F32, name="step%d" % t)
             first = H if t == ORDER[0] else 0
-            stop = N - LATE if t == ORDER[-1] else N
-            nc.scalar.activation(steps[t][:, first:stop], banks[t][:, first:stop], COPY, scale=-LR)
+            nc.scalar.activation(steps[t][:, first:N], banks[t][:, first:N], COPY, scale=-LR)
 
-        vector_pairs = pool.tile([P, 2, 2, PASS, 2], BF16, name="vector_pairs")
-        scalar_pairs = [pool.tile([P, 2, hi - lo, 2], BF16, name="pairs%d" % lo) for lo, hi in SCALAR_CHUNKS]
-        chunks = [(0, PASS), (PASS, 2 * PASS)] + SCALAR_CHUNKS
-        pairs = [vector_pairs[:, 0], vector_pairs[:, 1]] + [tile[:] for tile in scalar_pairs]
-        woven = [pool.tile([P, hi - lo, LANES], BF16, name="woven%d" % lo, align_bytes=64) for lo, hi in chunks]
+        rows = pool.tile([P, BLOCKS, LANES, BLOCK], BF16, name="rows")
+        pairs = pool.tile([P, BLOCKS, 2, BLOCK, 2], BF16, name="pairs")
 
-        def round_chunk(copy, t, c):
-            lo, hi = chunks[c]
-            copy(out=pairs[c][:, t // 2, :, t % 2], in_=table[t][:, lo:hi])
+        def round_rows(copy, t, lo, hi):
+            copy(
+                out=rows[:, lo:hi, t, :],
+                in_=table[t][:, lo * BLOCK : hi * BLOCK].rearrange("p (k c) -> p k c", c=BLOCK),
+            )
+
+        def round_pairs(t, lo, hi):
+            nc.scalar.copy(
+                out=pairs[:, lo:hi, t // 2, :, t % 2],
+                in_=table[t][:, (BLOCKS + lo) * BLOCK : (BLOCKS + hi) * BLOCK].rearrange("p (k c) -> p k c", c=BLOCK),
+            )
 
         for t in ORDER:
             if t == ORDER[0]:
@@ -254,20 +265,24 @@ def tile_attend_ghub_pl_sgd_kernel(tc, xT, wT, y, wt, xm, offs, out_0, out_1, ou
                 nc.vector.tensor_tensor(table[t][:].indirect(offsets[:]), decayed[t][:], steps[t][:], ALU.add)
             nc.sync.dma_start(out=out_rows[:, t, :], in_=table[t][:])
             if t != ORDER[-1]:
-                nc.scalar.copy(
-                    out=vector_pairs[:, :, t // 2, :, t % 2],
-                    in_=table[t][:, 0 : 2 * PASS].rearrange("p (c i) -> p c i", c=2),
-                )
-                for c in range(2, len(chunks)):
-                    round_chunk(nc.scalar.copy, t, c)
-            if t == ORDER[0]:
-                last = ORDER[-1]
-                nc.scalar.activation(steps[last][:, N - LATE : N], banks[last][:, N - LATE : N], COPY, scale=-LR)
+                round_pairs(t, 0, BLOCKS)
+                round_rows(nc.scalar.copy, t, 0, BLOCKS)
 
         out_scales = pool.tile([P, T // 2], U8, name="out_scales", align_bytes=64)
+        chunks = [(0, 1), (1, 2), (2, 4), (4, 6), (6, 7), (7, 8)]
+        woven = [
+            pool.tile([P, (hi - lo) * BLOCK, LANES], BF16, name="woven%d" % lo, align_bytes=64) for lo, hi in chunks
+        ]
+
+        def weave(c):
+            lo, hi = chunks[c]
+            if lo < BLOCKS:
+                weave_rows(nc.vector.tensor_copy, woven[c][:], rows[:, lo:hi])
+            else:
+                weave_words(nc.scalar.copy, woven[c][:], pairs[:, lo - BLOCKS : hi - BLOCKS])
 
         def quantize_out(c):
-            lo, hi = chunks[c]
+            lo, hi = chunks[c][0] * BLOCK, chunks[c][1] * BLOCK
             codes = pool.tile([P, hi - lo], U32, name="out_codes%d" % c, align_bytes=64)
             group = lo // (T // 2)
             nc.vector.quantize_mx(
@@ -278,17 +293,20 @@ def tile_attend_ghub_pl_sgd_kernel(tc, xT, wT, y, wt, xm, offs, out_0, out_1, ou
             nc.sync.dma_start(out=words_out[:, lo:hi], in_=codes[:].bitcast(I32))
 
         last = ORDER[-1]
-        for c in range(2):
-            round_chunk(nc.vector.tensor_copy, last, c)
-        for c in range(2):
-            weave_words(nc.vector.tensor_copy, woven[c], pairs[c])
-        round_chunk(nc.scalar.copy, last, 2)
-        round_chunk(nc.scalar.copy, last, 3)
-        weave_words(nc.scalar.copy, woven[2], pairs[2])
-        round_chunk(nc.scalar.copy, last, 4)
-        weave_words(nc.scalar.copy, woven[3], pairs[3])
-        weave_words(nc.scalar.copy, woven[4], pairs[4])
-        for c in range(len(chunks)):
+        round_rows(nc.vector.tensor_copy, last, 0, 1)
+        round_rows(nc.vector.tensor_copy, last, 1, 2)
+        round_rows(nc.scalar.copy, last, 2, 4)
+        round_pairs(last, 0, 2)
+        round_pairs(last, 2, 3)
+        weave(3)
+        round_pairs(last, 3, 4)
+        weave(4)
+        weave(5)
+        weave(0)
+        weave(1)
+        quantize_out(0)
+        weave(2)
+        for c in range(1, len(chunks)):
             quantize_out(c)
         for q in range(4):
             queue = nc.scalar if q % 2 else nc.sync

@@ -19,19 +19,11 @@ COPY = mybir.ActivationFunctionType.Copy
 
 P = 128
 LANES = 4
-HALF = 64
 H = N // 2
 PASS = 512
 ORDER = [0, 1, 2, 3]
 BLOCK = 256
 BLOCKS = 4
-
-
-def deal_copy(copy, dealt, raw, first, lo, hi):
-    copy(
-        out=dealt[:, :, lo:hi, :].rearrange("p (u e) s j -> p u s j e", e=2),
-        in_=raw[:, :, LANES * (lo - first) : LANES * (hi - first)].rearrange("p j (s u e) -> p u s j e", u=2, e=2),
-    )
 
 
 def weave_words(copy, woven, pairs):
@@ -53,9 +45,9 @@ def tile_attend_ghub_pl_sgd_kernel(tc, xT, wT, y, wt, xm, offs, out_0, out_1, ou
     w_rows = wT.rearrange("(p t) c -> p t c", t=LANES)
     out_rows = out_0.rearrange("(p t) c -> p t c", t=LANES)
     x_rows = xT[0].rearrange("(p j) r -> p j r", j=LANES)
-    xm_rows = xm[0].rearrange("(p j) d -> p j d", j=LANES)
-    y_rows = y[0].rearrange("(p t) i -> p t i", t=LANES)
-    wt_rows = wt[0].rearrange("(p t) o -> p (t o)", t=LANES)
+    xm_rows = xm[0].rearrange("(b t i) d -> t b i d", t=LANES, i=8)
+    y_rows = y[0].rearrange("(b t i) n -> t b i n", t=LANES, i=8)
+    wt_rows = wt[0].rearrange("(b t i) o -> t b i o", t=LANES, i=8)
     words_out = out_1[0].rearrange("p c l -> p (c l)").bitcast(I32)
     scales_out = out_2[0].bitcast(I32)
 
@@ -67,93 +59,125 @@ def tile_attend_ghub_pl_sgd_kernel(tc, xT, wT, y, wt, xm, offs, out_0, out_1, ou
         source = [pool.tile([P, T], F32, name="source%d" % t) for t in range(LANES)]
         table = [pool.tile([P, T], F32, name="table%d" % t) for t in range(LANES)]
         x_raw = pool.tile([P, LANES, R], F32, name="x_raw")
-        xm_raw = [pool.tile([P, LANES, D // 2], F32, name="xm_raw%d" % h) for h in range(2)]
-        y_raw = [pool.tile([P, N], F32, name="y_raw%d" % t, align_bytes=64) for t in range(LANES)]
-        weight = pool.tile([P, LANES], F32, name="weight")
+        xm_raw = pool.tile([P, LANES, D], F32, name="xm_raw")
+        y_raw = [pool.tile([P, N], F32, name="y_raw%d" % t) for t in range(LANES)]
+        padded_weight = pool.tile([P, LANES, 8], F32, name="padded_weight")
+        weight = [padded_weight[:, t, 0:1] for t in range(LANES)]
 
-        nc.sync.dma_start(out=x_raw[:], in_=x_rows)
+        nc.sync.dma_start(out=source[0][:], in_=w_rows[:, 0, :])
         nc.sync.dma_start(offsets[:], offs)
-        nc.scalar.dma_start(out=weight[:], in_=wt_rows)
-        for t in range(LANES):
+        with nc.allow_non_contiguous_dma(reason="one weight a partition"):
+            for t in range(LANES):
+                nc.sync.dma_start(out=weight[t], in_=wt_rows[t])
+        for t in range(1, LANES):
             nc.sync.dma_start(out=source[t][:], in_=w_rows[:, t, :])
+        nc.sync.dma_start(out=x_raw[:], in_=x_rows)
         for t in range(LANES):
-            nc.sync.dma_start(out=y_raw[t][:], in_=y_rows[:, t, :])
-        for h in range(2):
-            nc.sync.dma_start(out=xm_raw[h][:], in_=xm_rows[:, :, h * D // 2 : (h + 1) * D // 2])
+            nc.sync.dma_start(out=y_raw[t][:], in_=y_rows[t])
+        for t in range(LANES):
+            nc.sync.dma_start(out=xm_raw[:, t, :], in_=xm_rows[t])
         for t in ORDER:
             nc.sync.dma_start(out=table[t][:], in_=w_rows[:, t, :])
 
         upper = pool.tile([P, LANES], F32, name="upper")
         lower = pool.tile([P, LANES], F32, name="lower")
-        nc.vector.scalar_tensor_tensor(upper[:], weight[:], -1.0, weight[:], ALU.mult, ALU.max)
-        nc.vector.scalar_tensor_tensor(lower[:], weight[:], -1.0, weight[:], ALU.mult, ALU.min)
+        weights = padded_weight[:, :, 0]
+        nc.vector.scalar_tensor_tensor(upper[:], weights, -1.0, weights, ALU.mult, ALU.max)
+        nc.vector.scalar_tensor_tensor(lower[:], weights, -1.0, weights, ALU.mult, ALU.min)
 
         g_codes = pool.tile([P, N], U32, name="g_codes", align_bytes=64)
         g_scales = pool.tile([P, N], U8, name="g_scales", align_bytes=64)
         nc.vector.memset(g_codes[:, H:N], 0)
         nc.vector.memset(g_scales[:, H:N].bitcast(U32), 0)
 
-        x16 = pool.tile([P, LANES, P, LANES], BF16, name="x16", align_bytes=64)
-        deal_copy(nc.scalar.copy, x16, x_raw, 0, 0, P)
-        x_codes = [pool.tile([P, P], U32, name="x_codes%d" % t, align_bytes=64) for t in range(LANES)]
-        x_scales = [pool.tile([P, P], U8, name="x_scales%d" % t, align_bytes=64) for t in range(LANES)]
-        for t in range(LANES):
-            nc.vector.quantize_mx(
-                out=x_codes[t][:].bitcast(E4M3),
-                scales=x_scales[t][:],
-                in_=x16[:, t, :, :].rearrange("p s j -> p (s j)"),
-            )
-
         halves = [slice(0, H), slice(H, N)]
         w16 = [pool.tile([P, H, LANES], BF16, name="w16_%d" % h, align_bytes=64) for h in range(2)]
         decayed = [pool.tile([P, N], F32, name="decayed%d" % t) for t in range(LANES)]
         keep = 1.0 - LR * WD
         for t in range(LANES - 1):
-            picked = pool.tile([P, N], F32, name="picked%d" % (t % 2))
+            picked = pool.tile([P, N], F32, name="picked%d" % t)
             nc.vector.tensor_copy(picked[:], source[t][:].indirect(offsets[:]))
             nc.scalar.copy(out=w16[0][:, :, t], in_=picked[:, halves[0]])
             copy = nc.scalar.copy if t < 2 else nc.vector.tensor_copy
             copy(out=w16[1][:, :, t], in_=picked[:, halves[1]])
             nc.vector.tensor_scalar(decayed[t][:], picked[:], keep, None, ALU.mult)
         t = LANES - 1
-        picked_halves = [pool.tile([P, H], F32, name="picked%d" % (1 - h)) for h in range(2)]
+        picked_halves = [pool.tile([P, H], F32, name="picked_half%d" % h) for h in range(2)]
         for h in range(2):
             listed = offsets[:, h * H // 16 : (h + 1) * H // 16]
             nc.vector.tensor_copy(picked_halves[h][:], source[t][:].indirect(listed))
         nc.scalar.copy(out=w16[0][:, :, t], in_=picked_halves[0][:])
-        nc.vector.tensor_scalar(decayed[t][:, halves[0]], picked_halves[0][:], keep, None, ALU.mult)
-        nc.vector.tensor_copy(out=w16[1][:, :, t], in_=picked_halves[1][:])
+        nc.scalar.copy(out=w16[1][:, :, t], in_=picked_halves[1][:])
 
-        scores = []
-        for h in range(2):
-            w_codes = pool.tile([P, H], U32, name="w_codes%d" % h, align_bytes=64)
-            w_scales = pool.tile([P, H], U8, name="w_scales%d" % h, align_bytes=64)
+        w_codes = [pool.tile([P, H], U32, name="w_codes0", align_bytes=64)]
+        w_scales = [pool.tile([P, H], U8, name="w_scales%d" % h, align_bytes=64) for h in range(2)]
+
+        def quantize_w(h):
             nc.vector.quantize_mx(
-                out=w_codes[:].bitcast(E4M3), scales=w_scales[:], in_=w16[h][:].rearrange("p i t -> p (i t)")
+                out=w_codes[h][:].bitcast(E4M3), scales=w_scales[h][:], in_=w16[h][:].rearrange("p i t -> p (i t)")
             )
-            banks = [psum.tile([P, 2, H], F32, name="scores%d_%d" % (h, u)) for u in range(2)]
-            for t in range(LANES):
-                nc.tensor.matmul_mx(
-                    out=banks[t // 2][:, t % 2, :],
-                    lhsT=x_codes[t][:].bitcast(E4M3),
-                    lhsT_scale=x_scales[t][:],
-                    rhs=w_codes[:].bitcast(E4M3),
-                    rhs_scale=w_scales[:],
-                    start=True,
-                    stop=True,
-                )
-            scores.append(banks)
 
-        nc.vector.tensor_scalar(decayed[LANES - 1][:, halves[1]], picked_halves[1][:], keep, None, ALU.mult)
+        nc.vector.tensor_scalar(decayed[t][:, halves[0]], picked_halves[0][:], keep, None, ALU.mult)
+        quantize_w(0)
+        nc.vector.tensor_scalar(decayed[t][:, halves[1]], picked_halves[1][:], keep, None, ALU.mult)
 
-        weighted_y = [pool.tile([P, LANES, H], F32, name="picked%d" % (1 - h)) for h in range(2)]
-        for h in range(2):
-            for t in range(LANES):
-                nc.scalar.activation(weighted_y[h][:, t, :], y_raw[t][:, halves[h]], COPY, scale=weight[:, t : t + 1])
+        x16 = [pool.tile([P, P, LANES], BF16, name="x16_%d" % t, align_bytes=64) for t in range(LANES)]
+        x_by_lane = x_raw[:].rearrange("p j (b t c i) -> p t b c j i", t=LANES, c=2, i=4)
+        x_codes = [pool.tile([P, P], U32, name="x_codes%d" % t, align_bytes=64) for t in range(LANES)]
+        x_scales = [pool.tile([P, P], U8, name="x_scales%d" % t, align_bytes=64) for t in range(LANES)]
+        scores = [
+            [psum.tile([P, H], F32, name="bank%d" % (LANES * h + t)) for t in range(LANES)] for h in range(2)
+        ]
+        weighted_y = [pool.tile([P, LANES, H], F32, name="weighted_y%d" % h) for h in range(2)]
 
-        xm16 = pool.tile([P, LANES, P, LANES], BF16, name="y_raw3", align_bytes=64)
-        for h in range(2):
-            deal_copy(nc.scalar.copy, xm16, xm_raw[h], h * HALF, h * HALF, (h + 1) * HALF)
+        def deal_x(copy, t):
+            copy(out=x16[t][:].rearrange("p (b c i) j -> p b c j i", c=2, i=4), in_=x_by_lane[:, t])
+
+        def quantize_x(t):
+            nc.vector.quantize_mx(
+                out=x_codes[t][:].bitcast(E4M3),
+                scales=x_scales[t][:],
+                in_=x16[t][:].rearrange("p s j -> p (s j)"),
+            )
+
+        def score(h, t):
+            nc.tensor.matmul_mx(
+                out=scores[h][t][:],
+                lhsT=x_codes[t][:].bitcast(E4M3),
+                lhsT_scale=x_scales[t][:],
+                rhs=w_codes[h][:].bitcast(E4M3),
+                rhs_scale=w_scales[h][:],
+                start=True,
+                stop=True,
+            )
+
+        def weigh_targets(h, t):
+            nc.scalar.activation(weighted_y[h][:, t, :], y_raw[t][:, halves[h]], COPY, scale=weight[t])
+
+        deal_x(nc.vector.tensor_copy, 0)
+        deal_x(nc.scalar.copy, 1)
+        quantize_x(0)
+        score(0, 0)
+        deal_x(nc.vector.tensor_copy, 2)
+        for t in range(1, LANES - 1):
+            quantize_x(t)
+            score(0, t)
+        w_codes.append(pool.tile([P, H], U32, name="x16_0", align_bytes=64))
+        quantize_w(1)
+        weigh_targets(0, 0)
+        weigh_targets(0, 1)
+        deal_x(nc.scalar.copy, 3)
+        weigh_targets(0, 2)
+        weigh_targets(0, 3)
+        for t in range(LANES):
+            weigh_targets(1, t)
+
+        xm16 = pool.tile([P, LANES, P, LANES], BF16, name="xm16", align_bytes=64)
+        for u in range(2):
+            nc.scalar.copy(
+                out=xm16[:, 2 * u : 2 * u + 2].rearrange("p e s j -> p s j e"),
+                in_=xm_raw[:].rearrange("p j (s u e) -> p u s j e", u=2, e=2)[:, u],
+            )
 
         g_rows = [pool.tile([P, 1, LANES, H], BF16, name="g_rows%d" % h) for h in range(2)]
         g16 = [pool.tile([P, H, LANES], BF16, name="g16_%d" % h, align_bytes=64) for h in range(2)]
@@ -164,8 +188,8 @@ def tile_attend_ghub_pl_sgd_kernel(tc, xT, wT, y, wt, xm, offs, out_0, out_1, ou
         def subtract_targets(h, t):
             nc.vector.scalar_tensor_tensor(
                 residual[t][:, halves[h]],
-                scores[h][t // 2][:, t % 2, :],
-                weight[:, t : t + 1],
+                scores[h][t][:],
+                weight[t],
                 weighted_y[h][:, t, :],
                 ALU.mult,
                 ALU.subtract,
@@ -209,7 +233,13 @@ def tile_attend_ghub_pl_sgd_kernel(tc, xT, wT, y, wt, xm, offs, out_0, out_1, ou
             return bank
 
         subtract_targets(0, 0)
-        for t in range(1, LANES):
+        subtract_targets(0, 1)
+        quantize_x(LANES - 1)
+        score(0, LANES - 1)
+        for t in range(LANES):
+            score(1, t)
+        clamp(0, 0)
+        for t in range(2, LANES):
             subtract_targets(0, t)
             clamp(0, t - 1)
         subtract_targets(1, 0)
@@ -223,11 +253,11 @@ def tile_attend_ghub_pl_sgd_kernel(tc, xT, wT, y, wt, xm, offs, out_0, out_1, ou
         subtract_targets(1, 3)
         clamp(1, 2)
         quantize_xm(ORDER[0])
-        early_bank = gradient(ORDER[0], "scores0_0")
+        early_bank = gradient(ORDER[0], "bank0")
         clamp(1, 3)
         quantize_xm(ORDER[1])
         weave_rows(nc.vector.tensor_copy, g16[1][:], g_rows[1][:])
-        early_step = pool.tile([P, H], F32, name="g_rows1")
+        early_step = pool.tile([P, H], F32, name="early_step")
         nc.scalar.activation(early_step[:], early_bank[:, halves[0]], COPY, scale=-LR)
         quantize_xm(ORDER[2])
         quantize_g(1)
@@ -236,7 +266,7 @@ def tile_attend_ghub_pl_sgd_kernel(tc, xT, wT, y, wt, xm, offs, out_0, out_1, ou
         banks = {}
         steps = {}
         for t in ORDER:
-            banks[t] = gradient(t, "gradient%d" % t)
+            banks[t] = gradient(t, "bank%d" % (t + 1))
             steps[t] = pool.tile([P, N], F32, name="step%d" % t)
             first = H if t == ORDER[0] else 0
             nc.scalar.activation(steps[t][:, first:N], banks[t][:, first:N], COPY, scale=-LR)

@@ -45,9 +45,9 @@ def tile_attend_ghub_pl_sgd_kernel(tc, xT, wT, y, wt, xm, offs, out_0, out_1, ou
     w_rows = wT.rearrange("(p t) c -> p t c", t=LANES)
     out_rows = out_0.rearrange("(p t) c -> p t c", t=LANES)
     x_rows = xT[0].rearrange("(p j) r -> p j r", j=LANES)
-    xm_rows = xm[0].rearrange("(b t i) d -> t b i d", t=LANES, i=8)
-    y_rows = y[0].rearrange("(b t i) n -> t b i n", t=LANES, i=8)
-    wt_rows = wt[0].rearrange("(b t i) o -> t b i o", t=LANES, i=8)
+    xm_rows = xm[0].rearrange("(p j) d -> p j d", j=LANES)
+    y_rows = y[0].rearrange("(p t) i -> p t i", t=LANES)
+    wt_rows = wt[0].rearrange("(p t) o -> p (t o)", t=LANES)
     words_out = out_1[0].rearrange("p c l -> p (c l)").bitcast(I32)
     scales_out = out_2[0].bitcast(I32)
 
@@ -61,29 +61,25 @@ def tile_attend_ghub_pl_sgd_kernel(tc, xT, wT, y, wt, xm, offs, out_0, out_1, ou
         x_raw = pool.tile([P, LANES, R], F32, name="x_raw")
         xm_raw = pool.tile([P, LANES, D], F32, name="xm_raw")
         y_raw = [pool.tile([P, N], F32, name="y_raw%d" % t) for t in range(LANES)]
-        padded_weight = pool.tile([P, LANES, 8], F32, name="padded_weight")
-        weight = [padded_weight[:, t, 0:1] for t in range(LANES)]
+        weights = pool.tile([P, LANES], F32, name="weights")
+        weight = [weights[:, t : t + 1] for t in range(LANES)]
 
         nc.sync.dma_start(out=source[0][:], in_=w_rows[:, 0, :])
         nc.sync.dma_start(offsets[:], offs)
-        with nc.allow_non_contiguous_dma(reason="one weight a partition"):
-            for t in range(LANES):
-                nc.sync.dma_start(out=weight[t], in_=wt_rows[t])
+        nc.scalar.dma_start(out=weights[:], in_=wt_rows)
         for t in range(1, LANES):
             nc.sync.dma_start(out=source[t][:], in_=w_rows[:, t, :])
         nc.sync.dma_start(out=x_raw[:], in_=x_rows)
         for t in range(LANES):
-            nc.sync.dma_start(out=y_raw[t][:], in_=y_rows[t])
-        for t in range(LANES):
-            nc.sync.dma_start(out=xm_raw[:, t, :], in_=xm_rows[t])
+            nc.sync.dma_start(out=y_raw[t][:], in_=y_rows[:, t, :])
+        nc.sync.dma_start(out=xm_raw[:], in_=xm_rows)
         for t in ORDER:
             nc.sync.dma_start(out=table[t][:], in_=w_rows[:, t, :])
 
         upper = pool.tile([P, LANES], F32, name="upper")
         lower = pool.tile([P, LANES], F32, name="lower")
-        weights = padded_weight[:, :, 0]
-        nc.vector.scalar_tensor_tensor(upper[:], weights, -1.0, weights, ALU.mult, ALU.max)
-        nc.vector.scalar_tensor_tensor(lower[:], weights, -1.0, weights, ALU.mult, ALU.min)
+        nc.vector.scalar_tensor_tensor(upper[:], weights[:], -1.0, weights[:], ALU.mult, ALU.max)
+        nc.vector.scalar_tensor_tensor(lower[:], weights[:], -1.0, weights[:], ALU.mult, ALU.min)
 
         g_codes = pool.tile([P, N], U32, name="g_codes", align_bytes=64)
         g_scales = pool.tile([P, N], U8, name="g_scales", align_bytes=64)
@@ -121,8 +117,8 @@ def tile_attend_ghub_pl_sgd_kernel(tc, xT, wT, y, wt, xm, offs, out_0, out_1, ou
         quantize_w(0)
         nc.vector.tensor_scalar(decayed[t][:, halves[1]], picked_halves[1][:], keep, None, ALU.mult)
 
-        x16 = [pool.tile([P, P, LANES], BF16, name="x16_%d" % t, align_bytes=64) for t in range(LANES)]
-        x_by_lane = x_raw[:].rearrange("p j (b t c i) -> p t b c j i", t=LANES, c=2, i=4)
+        x16 = [pool.tile([P, 2, P, LANES], BF16, name="x16_%d" % u, align_bytes=64) for u in range(2)]
+        x_by_pair = x_raw[:].rearrange("p j (s u e) -> p u s j e", u=2, e=2)
         x_codes = [pool.tile([P, P], U32, name="x_codes%d" % t, align_bytes=64) for t in range(LANES)]
         x_scales = [pool.tile([P, P], U8, name="x_scales%d" % t, align_bytes=64) for t in range(LANES)]
         scores = [
@@ -130,14 +126,14 @@ def tile_attend_ghub_pl_sgd_kernel(tc, xT, wT, y, wt, xm, offs, out_0, out_1, ou
         ]
         weighted_y = [pool.tile([P, LANES, H], F32, name="weighted_y%d" % h) for h in range(2)]
 
-        def deal_x(copy, t):
-            copy(out=x16[t][:].rearrange("p (b c i) j -> p b c j i", c=2, i=4), in_=x_by_lane[:, t])
+        def deal_x(copy, u, lo, hi):
+            copy(out=x16[u][:, :, lo:hi].rearrange("p e s j -> p s j e"), in_=x_by_pair[:, u, lo:hi])
 
         def quantize_x(t):
             nc.vector.quantize_mx(
                 out=x_codes[t][:].bitcast(E4M3),
                 scales=x_scales[t][:],
-                in_=x16[t][:].rearrange("p s j -> p (s j)"),
+                in_=x16[t // 2][:, t % 2].rearrange("p s j -> p (s j)"),
             )
 
         def score(h, t):
@@ -154,19 +150,16 @@ def tile_attend_ghub_pl_sgd_kernel(tc, xT, wT, y, wt, xm, offs, out_0, out_1, ou
         def weigh_targets(h, t):
             nc.scalar.activation(weighted_y[h][:, t, :], y_raw[t][:, halves[h]], COPY, scale=weight[t])
 
-        deal_x(nc.vector.tensor_copy, 0)
-        deal_x(nc.scalar.copy, 1)
-        quantize_x(0)
-        score(0, 0)
-        deal_x(nc.vector.tensor_copy, 2)
-        for t in range(1, LANES - 1):
+        deal_x(nc.vector.tensor_copy, 0, 0, P)
+        deal_x(nc.scalar.copy, 1, 0, P // 2)
+        for t in range(2):
             quantize_x(t)
             score(0, t)
         w_codes.append(pool.tile([P, H], U32, name="x16_0", align_bytes=64))
         quantize_w(1)
         weigh_targets(0, 0)
         weigh_targets(0, 1)
-        deal_x(nc.scalar.copy, 3)
+        deal_x(nc.scalar.copy, 1, P // 2, P)
         weigh_targets(0, 2)
         weigh_targets(0, 3)
         for t in range(LANES):
@@ -234,8 +227,9 @@ def tile_attend_ghub_pl_sgd_kernel(tc, xT, wT, y, wt, xm, offs, out_0, out_1, ou
 
         subtract_targets(0, 0)
         subtract_targets(0, 1)
-        quantize_x(LANES - 1)
-        score(0, LANES - 1)
+        for t in range(2, LANES):
+            quantize_x(t)
+            score(0, t)
         for t in range(LANES):
             score(1, t)
         clamp(0, 0)

@@ -66,8 +66,9 @@ def tile_attend_ghub_pl_sgd_kernel(tc, xT, wT, y, wt, xm, offs, out_0, out_1, ou
 
         nc.sync.dma_start(out=source[0][:], in_=w_rows[:, 0, :])
         nc.sync.dma_start(offsets[:], offs)
-        nc.scalar.dma_start(out=weights[:], in_=wt_rows)
-        for t in range(1, LANES):
+        nc.sync.dma_start(out=source[1][:], in_=w_rows[:, 1, :])
+        nc.sync.dma_start(out=weights[:], in_=wt_rows)
+        for t in range(2, LANES):
             nc.sync.dma_start(out=source[t][:], in_=w_rows[:, t, :])
         nc.sync.dma_start(out=x_raw[:], in_=x_rows)
         for t in range(LANES):
@@ -90,13 +91,14 @@ def tile_attend_ghub_pl_sgd_kernel(tc, xT, wT, y, wt, xm, offs, out_0, out_1, ou
         w16 = [pool.tile([P, H, LANES], BF16, name="w16_%d" % h, align_bytes=64) for h in range(2)]
         decayed = [pool.tile([P, N], F32, name="decayed%d" % t) for t in range(LANES)]
         keep = 1.0 - LR * WD
+        picked = [pool.tile([P, N], F32, name="picked%d" % t) for t in range(LANES - 1)]
         for t in range(LANES - 1):
-            picked = pool.tile([P, N], F32, name="picked%d" % t)
-            nc.vector.tensor_copy(picked[:], source[t][:].indirect(offsets[:]))
-            nc.scalar.copy(out=w16[0][:, :, t], in_=picked[:, halves[0]])
+            nc.vector.tensor_copy(picked[t][:], source[t][:].indirect(offsets[:]))
+            nc.scalar.copy(out=w16[0][:, :, t], in_=picked[t][:, halves[0]])
             copy = nc.scalar.copy if t < 2 else nc.vector.tensor_copy
-            copy(out=w16[1][:, :, t], in_=picked[:, halves[1]])
-            nc.vector.tensor_scalar(decayed[t][:], picked[:], keep, None, ALU.mult)
+            copy(out=w16[1][:, :, t], in_=picked[t][:, halves[1]])
+            first = H if t == 0 else 0
+            nc.vector.tensor_scalar(decayed[t][:, first:N], picked[t][:, first:N], keep, None, ALU.mult)
         t = LANES - 1
         picked_halves = [pool.tile([P, H], F32, name="picked_half%d" % h) for h in range(2)]
         for h in range(2):
@@ -165,22 +167,26 @@ def tile_attend_ghub_pl_sgd_kernel(tc, xT, wT, y, wt, xm, offs, out_0, out_1, ou
         for t in range(LANES):
             weigh_targets(1, t)
 
-        xm16 = pool.tile([P, LANES, P, LANES], BF16, name="xm16", align_bytes=64)
+        xm16 = [pool.tile([P, 2, P, LANES], BF16, name="xm16_%d" % u, align_bytes=64) for u in range(2)]
         for u in range(2):
             nc.scalar.copy(
-                out=xm16[:, 2 * u : 2 * u + 2].rearrange("p e s j -> p s j e"),
+                out=xm16[u][:].rearrange("p e s j -> p s j e"),
                 in_=xm_raw[:].rearrange("p j (s u e) -> p u s j e", u=2, e=2)[:, u],
             )
 
-        g_rows = [pool.tile([P, 1, LANES, H], BF16, name="g_rows%d" % h) for h in range(2)]
-        g16 = [pool.tile([P, H, LANES], BF16, name="g16_%d" % h, align_bytes=64) for h in range(2)]
-        residual = [pool.tile([P, N], F32, name="residual%d" % t) for t in range(LANES)]
-        xm_codes = [pool.tile([P, P], U32, name="xm_codes%d" % t, align_bytes=64) for t in range(LANES)]
-        xm_scales = [pool.tile([P, P], U8, name="xm_scales%d" % t, align_bytes=64) for t in range(LANES)]
+        g_rows = [pool.tile([P, 1, LANES, H], BF16, name="g_rows0")]
+        pieces = [(0, H), (H, H + H // 2), (H + H // 2, N)]
+        g16 = [pool.tile([P, hi - lo, LANES], BF16, name="g16_%d" % lo, align_bytes=64) for lo, hi in pieces]
+        residual = [
+            [pool.tile([P, H], F32, name="residual%d_%d" % (h, t), align_bytes=64) for t in range(LANES)]
+            for h in range(2)
+        ]
+        xm_codes = []
+        xm_scales = []
 
         def subtract_targets(h, t):
             nc.vector.scalar_tensor_tensor(
-                residual[t][:, halves[h]],
+                residual[h][t][:],
                 scores[h][t][:],
                 weight[t],
                 weighted_y[h][:, t, :],
@@ -188,36 +194,48 @@ def tile_attend_ghub_pl_sgd_kernel(tc, xT, wT, y, wt, xm, offs, out_0, out_1, ou
                 ALU.subtract,
             )
 
-        def clamp(h, t):
+        def clamp(h, t, lo=0, hi=H):
             nc.vector.tensor_scalar(
-                g_rows[h][:, 0, t, :],
-                residual[t][:, halves[h]],
+                g_rows[h][:, 0, t, lo:hi],
+                residual[h][t][:, lo:hi],
                 lower[:, t : t + 1],
                 upper[:, t : t + 1],
                 ALU.max,
                 ALU.min,
             )
 
-        def quantize_g(h):
-            nc.vector.quantize_mx(
-                out=g_codes[:, halves[h]].bitcast(E5M2),
-                scales=g_scales[:, halves[h]],
-                in_=g16[h][:].rearrange("p i t -> p (i t)"),
+        def weave_g(k):
+            lo, hi = pieces[k]
+            h = lo // H
+            nc.vector.tensor_copy(
+                out=g16[k][:].rearrange("p (c i) t -> p c t i", i=4),
+                in_=g_rows[h][:, 0, :, lo - h * H : hi - h * H].rearrange("p t (c i) -> p c t i", i=4),
             )
 
-        def quantize_xm(t):
+        def quantize_g(k):
+            lo, hi = pieces[k]
             nc.vector.quantize_mx(
-                out=xm_codes[t][:].bitcast(E4M3),
-                scales=xm_scales[t][:],
-                in_=xm16[:, t, :, :].rearrange("p s j -> p (s j)"),
+                out=g_codes[:, lo:hi].bitcast(E5M2),
+                scales=g_scales[:, lo:hi],
+                in_=g16[k][:].rearrange("p i t -> p (i t)"),
             )
+
+        def quantize_xm(u, name):
+            codes = pool.tile([P, 2 * P], U32, name=name, align_bytes=64)
+            scales = pool.tile([P, 2 * P], U8, name="xm_scales%d" % u, align_bytes=64)
+            nc.vector.quantize_mx(
+                out=codes[:].bitcast(E4M3), scales=scales[:], in_=xm16[u][:].rearrange("p e s j -> p (e s j)")
+            )
+            for e in range(2):
+                xm_codes.append(codes[:, e * P : (e + 1) * P])
+                xm_scales.append(scales[:, e * P : (e + 1) * P])
 
         def gradient(t, name):
             bank = psum.tile([P, N], F32, name=name)
             nc.tensor.matmul_mx(
                 out=bank[:],
-                lhsT=xm_codes[t][:].bitcast(E4M3),
-                lhsT_scale=xm_scales[t][:],
+                lhsT=xm_codes[t].bitcast(E4M3),
+                lhsT_scale=xm_scales[t],
                 rhs=g_codes[:].bitcast(E5M2),
                 rhs_scale=g_scales[:],
                 start=True,
@@ -239,31 +257,43 @@ def tile_attend_ghub_pl_sgd_kernel(tc, xT, wT, y, wt, xm, offs, out_0, out_1, ou
         subtract_targets(1, 0)
         clamp(0, LANES - 1)
         subtract_targets(1, 1)
-        weave_rows(nc.vector.tensor_copy, g16[0][:], g_rows[0][:])
-        clamp(1, 0)
+        weave_g(0)
         subtract_targets(1, 2)
         quantize_g(0)
-        clamp(1, 1)
-        subtract_targets(1, 3)
-        clamp(1, 2)
-        quantize_xm(ORDER[0])
+        quantize_xm(0, "xm_codes0")
         early_bank = gradient(ORDER[0], "bank0")
-        clamp(1, 3)
-        quantize_xm(ORDER[1])
-        weave_rows(nc.vector.tensor_copy, g16[1][:], g_rows[1][:])
-        early_step = pool.tile([P, H], F32, name="early_step")
+        subtract_targets(1, 3)
+        g_rows.append(pool.tile([P, 1, LANES, H], BF16, name="xm16_0", align_bytes=64))
+        for t in range(LANES - 1):
+            clamp(1, t)
+        quarters = [(0, H // 2), (H // 2, H)]
+        for lo, hi in quarters:
+            clamp(1, LANES - 1, lo, hi)
+        weave_g(1)
+        weave_g(2)
+        early_step = pool.tile([P, H], F32, name="residual1_3", align_bytes=64)
         nc.scalar.activation(early_step[:], early_bank[:, halves[0]], COPY, scale=-LR)
-        quantize_xm(ORDER[2])
         quantize_g(1)
-        quantize_xm(ORDER[3])
+        early_decayed = pool.tile([P, H], F32, name="g16_%d" % H, align_bytes=64)
+        nc.vector.tensor_scalar(early_decayed[:], picked[0][:, halves[0]], keep, None, ALU.mult)
+        quantize_g(2)
 
-        banks = {}
-        steps = {}
-        for t in ORDER:
-            banks[t] = gradient(t, "bank%d" % (t + 1))
-            steps[t] = pool.tile([P, N], F32, name="step%d" % t)
-            first = H if t == ORDER[0] else 0
-            nc.scalar.activation(steps[t][:, first:N], banks[t][:, first:N], COPY, scale=-LR)
+        steps = [pool.tile([P, N], F32, name="step%d" % t) for t in range(LANES)]
+
+        def take_step(t, first):
+            bank = gradient(t, "bank%d" % (t + 1))
+            nc.scalar.activation(steps[t][:, first:N], bank[:, first:N], COPY, scale=-LR)
+
+        def scatter(t, slots, kept, step):
+            listed = offsets[:, slots.start // 16 : slots.stop // 16]
+            nc.vector.tensor_tensor(table[t][:].indirect(listed), kept, step, ALU.add)
+
+        take_step(0, H)
+        take_step(1, 0)
+        scatter(0, halves[0], early_decayed[:], early_step[:])
+        quantize_xm(1, "g16_%d" % (H + H // 2))
+        for t in range(2, LANES):
+            take_step(t, 0)
 
         rows = pool.tile([P, BLOCKS, LANES, BLOCK], BF16, name="rows")
         pairs = pool.tile([P, BLOCKS, 2, BLOCK, 2], BF16, name="pairs")
@@ -281,12 +311,8 @@ def tile_attend_ghub_pl_sgd_kernel(tc, xT, wT, y, wt, xm, offs, out_0, out_1, ou
             )
 
         for t in ORDER:
-            if t == ORDER[0]:
-                for h, step in enumerate([early_step[:], steps[t][:, halves[1]]]):
-                    listed = offsets[:, h * H // 16 : (h + 1) * H // 16]
-                    nc.vector.tensor_tensor(table[t][:].indirect(listed), decayed[t][:, halves[h]], step, ALU.add)
-            else:
-                nc.vector.tensor_tensor(table[t][:].indirect(offsets[:]), decayed[t][:], steps[t][:], ALU.add)
+            slots = halves[1] if t == 0 else slice(0, N)
+            scatter(t, slots, decayed[t][:, slots], steps[t][:, slots])
             nc.sync.dma_start(out=out_rows[:, t, :], in_=table[t][:])
             if t != ORDER[-1]:
                 round_pairs(t, 0, BLOCKS)

@@ -318,7 +318,7 @@ def tile_attend_ghub_pl_sgd_kernel(tc, xT, wT, y, wt, xm, offs, out_0, out_1, ou
                 round_pairs(t, 0, BLOCKS)
                 round_rows(nc.scalar.copy, t, 0, BLOCKS)
 
-        out_scales = pool.tile([P, T // 2], U8, name="out_scales", align_bytes=64)
+        out_scales = pool.tile([P, T // 4], U8, name="out_scales", align_bytes=64)
         chunks = [(0, 1), (1, 2), (2, 4), (4, 6), (6, 7), (7, 8)]
         woven = [
             pool.tile([P, (hi - lo) * BLOCK, LANES], BF16, name="woven%d" % lo, align_bytes=64) for lo, hi in chunks
@@ -332,15 +332,16 @@ def tile_attend_ghub_pl_sgd_kernel(tc, xT, wT, y, wt, xm, offs, out_0, out_1, ou
                 weave_words(nc.scalar.copy, woven[c][:], pairs[:, lo - BLOCKS : hi - BLOCKS])
 
         def quantize_out(c):
-            lo, hi = chunks[c][0] * BLOCK, chunks[c][1] * BLOCK
-            codes = pool.tile([P, hi - lo], U32, name="out_codes%d" % c, align_bytes=64)
-            group = lo // (T // 2)
-            nc.vector.quantize_mx(
-                out=codes[:].bitcast(E4M3),
-                scales=out_scales[4 * group : P, lo - group * T // 2 : hi - group * T // 2],
-                in_=woven[c][:].rearrange("p c l -> p (c l)"),
-            )
-            nc.sync.dma_start(out=words_out[:, lo:hi], in_=codes[:].bitcast(I32))
+            first, stop = chunks[c]
+            codes = pool.tile([P, (stop - first) * BLOCK], U32, name="out_codes%d" % c, align_bytes=64)
+            for k in range(first, stop):
+                here = slice((k - first) * BLOCK, (k - first + 1) * BLOCK)
+                nc.vector.quantize_mx(
+                    out=codes[:, here].bitcast(E4M3),
+                    scales=out_scales[4 * (k // 2) : P, (k % 2) * BLOCK : (k % 2 + 1) * BLOCK],
+                    in_=woven[c][:, here].rearrange("p c l -> p (c l)"),
+                )
+            nc.sync.dma_start(out=words_out[:, first * BLOCK : stop * BLOCK], in_=codes[:].bitcast(I32))
 
         last = ORDER[-1]
         round_rows(nc.vector.tensor_copy, last, 0, 1)
@@ -361,6 +362,6 @@ def tile_attend_ghub_pl_sgd_kernel(tc, xT, wT, y, wt, xm, offs, out_0, out_1, ou
         for q in range(4):
             queue = nc.scalar if q % 2 else nc.sync
             queue.dma_start(
-                out=scales_out[4 * q : 4 * q + 4, :].rearrange("f (g w) -> g f w", g=2),
-                in_=out_scales[32 * q : 32 * q + 8, :].bitcast(I32),
+                out=scales_out[4 * q : 4 * q + 4, :].rearrange("f (g w) -> g f w", g=4),
+                in_=out_scales[32 * q : 32 * q + 16, :].bitcast(I32),
             )

@@ -59,33 +59,30 @@ def tile_attend_ghub_pl_sgd_kernel(tc, xT, wT, y, wt, xm, offs, out_0, out_1, ou
         source = [pool.tile([P, T], F32, name="source%d" % t) for t in range(LANES)]
         table = [pool.tile([P, T], F32, name="table%d" % t) for t in range(LANES)]
         x_raw = pool.tile([P, LANES, R], F32, name="x_raw")
-        xm_raw = pool.tile([P, LANES, D], F32, name="xm_raw")
-        y_raw = [pool.tile([P, N], F32, name="y_raw%d" % t) for t in range(LANES)]
+        xm_raw = pool.tile([P, LANES, D], F32, name="xm_raw", align_bytes=64)
+        y_pairs = [pool.tile([P, 2, N], F32, name="y_pair%d" % u) for u in range(2)]
+        y_raw = [y_pairs[t // 2][:, t % 2, :] for t in range(LANES)]
         weights = pool.tile([P, LANES], F32, name="weights")
         weight = [weights[:, t : t + 1] for t in range(LANES)]
 
         nc.sync.dma_start(out=source[0][:], in_=w_rows[:, 0, :])
         nc.sync.dma_start(offsets[:], offs)
         nc.sync.dma_start(out=source[1][:], in_=w_rows[:, 1, :])
-        nc.sync.dma_start(out=weights[:], in_=wt_rows)
         for t in range(2, LANES):
             nc.sync.dma_start(out=source[t][:], in_=w_rows[:, t, :])
         nc.sync.dma_start(out=x_raw[:], in_=x_rows)
-        for t in range(LANES):
-            nc.sync.dma_start(out=y_raw[t][:], in_=y_rows[:, t, :])
+        nc.sync.dma_start(out=weights[:], in_=wt_rows)
+        for u in range(2):
+            nc.sync.dma_start(out=y_pairs[u][:], in_=y_rows[:, 2 * u : 2 * u + 2, :])
         nc.sync.dma_start(out=xm_raw[:], in_=xm_rows)
-        for t in ORDER:
+        for t in ORDER[1:]:
             nc.sync.dma_start(out=table[t][:], in_=w_rows[:, t, :])
 
-        upper = pool.tile([P, LANES], F32, name="upper")
-        lower = pool.tile([P, LANES], F32, name="lower")
-        nc.vector.scalar_tensor_tensor(upper[:], weights[:], -1.0, weights[:], ALU.mult, ALU.max)
-        nc.vector.scalar_tensor_tensor(lower[:], weights[:], -1.0, weights[:], ALU.mult, ALU.min)
 
-        g_codes = pool.tile([P, N], U32, name="g_codes", align_bytes=64)
-        g_scales = pool.tile([P, N], U8, name="g_scales", align_bytes=64)
-        nc.vector.memset(g_codes[:, H:N], 0)
-        nc.vector.memset(g_scales[:, H:N].bitcast(U32), 0)
+        g_codes = pool.tile([P, H + N], U32, name="g_codes", align_bytes=64)
+        g_scales = pool.tile([P, H + N], U8, name="g_scales", align_bytes=64)
+        nc.vector.memset(g_codes[:, 0:H], 0)
+        nc.vector.memset(g_scales[:, 0:H].bitcast(U32), 0)
 
         halves = [slice(0, H), slice(H, N)]
         w16 = [pool.tile([P, H, LANES], BF16, name="w16_%d" % h, align_bytes=64) for h in range(2)]
@@ -97,15 +94,17 @@ def tile_attend_ghub_pl_sgd_kernel(tc, xT, wT, y, wt, xm, offs, out_0, out_1, ou
             nc.scalar.copy(out=w16[0][:, :, t], in_=picked[t][:, halves[0]])
             copy = nc.scalar.copy if t < 2 else nc.vector.tensor_copy
             copy(out=w16[1][:, :, t], in_=picked[t][:, halves[1]])
-            first = H if t == 0 else 0
-            nc.vector.tensor_scalar(decayed[t][:, first:N], picked[t][:, first:N], keep, None, ALU.mult)
+            nc.vector.tensor_scalar(decayed[t][:], picked[t][:], keep, None, ALU.mult)
+            if t < 2:
+                columns = slice(t * T // 2, (t + 1) * T // 2)
+                nc.vector.tensor_copy(table[0][:, columns], source[0][:, columns])
         t = LANES - 1
         picked_halves = [pool.tile([P, H], F32, name="picked_half%d" % h) for h in range(2)]
         for h in range(2):
             listed = offsets[:, h * H // 16 : (h + 1) * H // 16]
             nc.vector.tensor_copy(picked_halves[h][:], source[t][:].indirect(listed))
         nc.scalar.copy(out=w16[0][:, :, t], in_=picked_halves[0][:])
-        nc.scalar.copy(out=w16[1][:, :, t], in_=picked_halves[1][:])
+        nc.vector.tensor_copy(out=w16[1][:, :, t], in_=picked_halves[1][:])
 
         w_codes = [pool.tile([P, H], U32, name="w_codes0", align_bytes=64)]
         w_scales = [pool.tile([P, H], U8, name="w_scales%d" % h, align_bytes=64) for h in range(2)]
@@ -115,9 +114,9 @@ def tile_attend_ghub_pl_sgd_kernel(tc, xT, wT, y, wt, xm, offs, out_0, out_1, ou
                 out=w_codes[h][:].bitcast(E4M3), scales=w_scales[h][:], in_=w16[h][:].rearrange("p i t -> p (i t)")
             )
 
-        nc.vector.tensor_scalar(decayed[t][:, halves[0]], picked_halves[0][:], keep, None, ALU.mult)
+        for h in range(2):
+            nc.scalar.activation(decayed[t][:, halves[h]], picked_halves[h][:], COPY, scale=keep)
         quantize_w(0)
-        nc.vector.tensor_scalar(decayed[t][:, halves[1]], picked_halves[1][:], keep, None, ALU.mult)
 
         x16 = [pool.tile([P, 2, P, LANES], BF16, name="x16_%d" % u, align_bytes=64) for u in range(2)]
         x_by_pair = x_raw[:].rearrange("p j (s u e) -> p u s j e", u=2, e=2)
@@ -153,28 +152,36 @@ def tile_attend_ghub_pl_sgd_kernel(tc, xT, wT, y, wt, xm, offs, out_0, out_1, ou
             nc.scalar.activation(weighted_y[h][:, t, :], y_raw[t][:, halves[h]], COPY, scale=weight[t])
 
         deal_x(nc.vector.tensor_copy, 0, 0, P)
-        deal_x(nc.scalar.copy, 1, 0, P // 2)
+        deal_x(nc.scalar.copy, 1, 0, P)
+        upper = pool.tile([P, LANES], F32, name="upper")
+        lower = pool.tile([P, LANES], F32, name="lower")
+        nc.vector.scalar_tensor_tensor(upper[:], weights[:], -1.0, weights[:], ALU.mult, ALU.max)
+        nc.vector.scalar_tensor_tensor(lower[:], weights[:], -1.0, weights[:], ALU.mult, ALU.min)
         for t in range(2):
             quantize_x(t)
             score(0, t)
         w_codes.append(pool.tile([P, H], U32, name="x16_0", align_bytes=64))
         quantize_w(1)
-        weigh_targets(0, 0)
-        weigh_targets(0, 1)
-        deal_x(nc.scalar.copy, 1, P // 2, P)
-        weigh_targets(0, 2)
-        weigh_targets(0, 3)
-        for t in range(LANES):
-            weigh_targets(1, t)
-
-        xm16 = [pool.tile([P, 2, P, LANES], BF16, name="xm16_%d" % u, align_bytes=64) for u in range(2)]
         for u in range(2):
+            for h in range(2):
+                for t in range(2 * u, 2 * u + 2):
+                    weigh_targets(h, t)
+
+        shared = pool.tile([P, 7 * H], BF16, name="shared", align_bytes=64)
+        xm16 = [shared[:, 3 * H : 7 * H], shared[:, 0 : 4 * H]]
+
+        def deal_xm(u):
             nc.scalar.copy(
-                out=xm16[u][:].rearrange("p e s j -> p s j e"),
+                out=xm16[u].rearrange("p (e s j) -> p s j e", e=2, j=LANES),
                 in_=xm_raw[:].rearrange("p j (s u e) -> p u s j e", u=2, e=2)[:, u],
             )
 
-        g_rows = [pool.tile([P, 1, LANES, H], BF16, name="g_rows0")]
+        deal_xm(0)
+
+        g_rows = [
+            pool.tile([P, 1, LANES, H], BF16, name="g_rows0"),
+            shared[:, 0 : 4 * H].rearrange("p (o t c) -> p o t c", o=1, t=LANES),
+        ]
         pieces = [(0, H), (H, H + H // 2), (H + H // 2, N)]
         g16 = [pool.tile([P, hi - lo, LANES], BF16, name="g16_%d" % lo, align_bytes=64) for lo, hi in pieces]
         residual = [
@@ -204,40 +211,41 @@ def tile_attend_ghub_pl_sgd_kernel(tc, xT, wT, y, wt, xm, offs, out_0, out_1, ou
                 ALU.min,
             )
 
-        def weave_g(k):
-            lo, hi = pieces[k]
+        def weave_g(copy, k, lo, hi):
+            first = pieces[k][0]
             h = lo // H
-            nc.vector.tensor_copy(
-                out=g16[k][:].rearrange("p (c i) t -> p c t i", i=4),
+            copy(
+                out=g16[k][:, lo - first : hi - first].rearrange("p (c i) t -> p c t i", i=4),
                 in_=g_rows[h][:, 0, :, lo - h * H : hi - h * H].rearrange("p t (c i) -> p c t i", i=4),
             )
 
         def quantize_g(k):
             lo, hi = pieces[k]
             nc.vector.quantize_mx(
-                out=g_codes[:, lo:hi].bitcast(E5M2),
-                scales=g_scales[:, lo:hi],
+                out=g_codes[:, H + lo : H + hi].bitcast(E5M2),
+                scales=g_scales[:, H + lo : H + hi],
                 in_=g16[k][:].rearrange("p i t -> p (i t)"),
             )
 
-        def quantize_xm(u, name):
-            codes = pool.tile([P, 2 * P], U32, name=name, align_bytes=64)
-            scales = pool.tile([P, 2 * P], U8, name="xm_scales%d" % u, align_bytes=64)
+        def quantize_xm(first, count):
+            codes = pool.tile([P, count * P], U32, name="xm_codes%d" % first, align_bytes=64)
+            scales = pool.tile([P, count * P], U8, name="xm_scales%d" % first, align_bytes=64)
+            start = (first % 2) * PASS
             nc.vector.quantize_mx(
-                out=codes[:].bitcast(E4M3), scales=scales[:], in_=xm16[u][:].rearrange("p e s j -> p (e s j)")
+                out=codes[:].bitcast(E4M3), scales=scales[:], in_=xm16[first // 2][:, start : start + count * PASS]
             )
-            for e in range(2):
+            for e in range(count):
                 xm_codes.append(codes[:, e * P : (e + 1) * P])
                 xm_scales.append(scales[:, e * P : (e + 1) * P])
 
-        def gradient(t, name):
+        def gradient(t, name, first=H):
             bank = psum.tile([P, N], F32, name=name)
             nc.tensor.matmul_mx(
                 out=bank[:],
                 lhsT=xm_codes[t].bitcast(E4M3),
                 lhsT_scale=xm_scales[t],
-                rhs=g_codes[:].bitcast(E5M2),
-                rhs_scale=g_scales[:],
+                rhs=g_codes[:, first : first + N].bitcast(E5M2),
+                rhs_scale=g_scales[:, first : first + N],
                 start=True,
                 stop=True,
             )
@@ -257,43 +265,42 @@ def tile_attend_ghub_pl_sgd_kernel(tc, xT, wT, y, wt, xm, offs, out_0, out_1, ou
         subtract_targets(1, 0)
         clamp(0, LANES - 1)
         subtract_targets(1, 1)
-        weave_g(0)
+        weave_g(nc.vector.tensor_copy, 0, 0, H)
         subtract_targets(1, 2)
         quantize_g(0)
-        quantize_xm(0, "xm_codes0")
-        early_bank = gradient(ORDER[0], "bank0")
         subtract_targets(1, 3)
-        g_rows.append(pool.tile([P, 1, LANES, H], BF16, name="xm16_0", align_bytes=64))
         for t in range(LANES - 1):
             clamp(1, t)
+        quantize_xm(0, 1)
+        early_bank = gradient(ORDER[0], "bank0", 0)
+        quantize_xm(1, 1)
         quarters = [(0, H // 2), (H // 2, H)]
         for lo, hi in quarters:
             clamp(1, LANES - 1, lo, hi)
-        weave_g(1)
-        weave_g(2)
+        weave_g(nc.scalar.copy, 1, *pieces[1])
+        weave_g(nc.vector.tensor_copy, 2, *pieces[2])
         early_step = pool.tile([P, H], F32, name="residual1_3", align_bytes=64)
-        nc.scalar.activation(early_step[:], early_bank[:, halves[0]], COPY, scale=-LR)
-        quantize_g(1)
-        early_decayed = pool.tile([P, H], F32, name="g16_%d" % H, align_bytes=64)
-        nc.vector.tensor_scalar(early_decayed[:], picked[0][:, halves[0]], keep, None, ALU.mult)
+        nc.scalar.activation(early_step[:], early_bank[:, halves[1]], COPY, scale=-LR)
+        deal_xm(1)
         quantize_g(2)
+        quantize_g(1)
 
-        steps = [pool.tile([P, N], F32, name="step%d" % t) for t in range(LANES)]
+        steps = []
 
-        def take_step(t, first):
-            bank = gradient(t, "bank%d" % (t + 1))
+        def take_step(t, bank, first, name):
+            steps.append(pool.tile([P, N], F32, name=name, align_bytes=64))
             nc.scalar.activation(steps[t][:, first:N], bank[:, first:N], COPY, scale=-LR)
 
         def scatter(t, slots, kept, step):
             listed = offsets[:, slots.start // 16 : slots.stop // 16]
             nc.vector.tensor_tensor(table[t][:].indirect(listed), kept, step, ALU.add)
 
-        take_step(0, H)
-        take_step(1, 0)
-        scatter(0, halves[0], early_decayed[:], early_step[:])
-        quantize_xm(1, "g16_%d" % (H + H // 2))
+        take_step(0, gradient(0, "bank1"), H, "step0")
+        take_step(1, gradient(1, "bank2"), 0, "step1")
+        scatter(0, halves[0], decayed[0][:, halves[0]], early_step[:])
+        quantize_xm(2, 2)
         for t in range(2, LANES):
-            take_step(t, 0)
+            take_step(t, gradient(t, "bank%d" % (t + 1)), 0, "step%d" % t)
 
         rows = pool.tile([P, BLOCKS, LANES, BLOCK], BF16, name="rows")
         pairs = pool.tile([P, BLOCKS, 2, BLOCK, 2], BF16, name="pairs")

@@ -86,25 +86,34 @@ def tile_attend_ghub_pl_sgd_kernel(tc, xT, wT, y, wt, xm, offs, out_0, out_1, ou
 
         halves = [slice(0, H), slice(H, N)]
         w16 = [pool.tile([P, H, LANES], BF16, name="w16_%d" % h, align_bytes=64) for h in range(2)]
-        decayed = [pool.tile([P, N], F32, name="decayed%d" % t) for t in range(LANES)]
+        decayed = [pool.tile([P, N], F32, name="decayed%d" % t) for t in range(LANES - 1)]
         keep = 1.0 - LR * WD
         picked = [pool.tile([P, N], F32, name="picked%d" % t) for t in range(LANES - 1)]
+
+        def round_shared(t, sources):
+            for h in range(2):
+                for q in range(2):
+                    copy = nc.scalar.copy if h == q else nc.vector.tensor_copy
+                    quarter = slice(q * H // 2, (q + 1) * H // 2)
+                    copy(out=w16[h][:, quarter, t], in_=sources[h][:, quarter])
+
         for t in range(LANES - 1):
             nc.vector.tensor_copy(picked[t][:], source[t][:].indirect(offsets[:]))
-            nc.scalar.copy(out=w16[0][:, :, t], in_=picked[t][:, halves[0]])
-            copy = nc.scalar.copy if t < 2 else nc.vector.tensor_copy
-            copy(out=w16[1][:, :, t], in_=picked[t][:, halves[1]])
-            nc.vector.tensor_scalar(decayed[t][:], picked[t][:], keep, None, ALU.mult)
             if t < 2:
+                for h in range(2):
+                    nc.scalar.copy(out=w16[h][:, :, t], in_=picked[t][:, halves[h]])
+                nc.vector.tensor_scalar(decayed[t][:], picked[t][:], keep, None, ALU.mult)
                 columns = slice(t * T // 2, (t + 1) * T // 2)
                 nc.vector.tensor_copy(table[0][:, columns], source[0][:, columns])
+            else:
+                round_shared(t, [picked[t][:, half] for half in halves])
+                nc.scalar.activation(decayed[t][:], picked[t][:], COPY, scale=keep)
         t = LANES - 1
         picked_halves = [pool.tile([P, H], F32, name="picked_half%d" % h) for h in range(2)]
         for h in range(2):
             listed = offsets[:, h * H // 16 : (h + 1) * H // 16]
             nc.vector.tensor_copy(picked_halves[h][:], source[t][:].indirect(listed))
-        nc.scalar.copy(out=w16[0][:, :, t], in_=picked_halves[0][:])
-        nc.vector.tensor_copy(out=w16[1][:, :, t], in_=picked_halves[1][:])
+        round_shared(t, picked_halves)
 
         w_codes = [pool.tile([P, H], U32, name="w_codes0", align_bytes=64)]
         w_scales = [pool.tile([P, H], U8, name="w_scales%d" % h, align_bytes=64) for h in range(2)]
@@ -114,8 +123,6 @@ def tile_attend_ghub_pl_sgd_kernel(tc, xT, wT, y, wt, xm, offs, out_0, out_1, ou
                 out=w_codes[h][:].bitcast(E4M3), scales=w_scales[h][:], in_=w16[h][:].rearrange("p i t -> p (i t)")
             )
 
-        for h in range(2):
-            nc.scalar.activation(decayed[t][:, halves[h]], picked_halves[h][:], COPY, scale=keep)
         quantize_w(0)
 
         x16 = [pool.tile([P, 2, P, LANES], BF16, name="x16_%d" % u, align_bytes=64) for u in range(2)]
@@ -166,6 +173,10 @@ def tile_attend_ghub_pl_sgd_kernel(tc, xT, wT, y, wt, xm, offs, out_0, out_1, ou
             for h in range(2):
                 for t in range(2 * u, 2 * u + 2):
                     weigh_targets(h, t)
+
+        decayed.append(pool.tile([P, N], F32, name="y_pair1"))
+        for h in range(2):
+            nc.scalar.activation(decayed[LANES - 1][:, halves[h]], picked_halves[h][:], COPY, scale=keep)
 
         shared = pool.tile([P, 7 * H], BF16, name="shared", align_bytes=64)
         xm16 = [shared[:, 3 * H : 7 * H], shared[:, 0 : 4 * H]]

@@ -24,6 +24,7 @@ PASS = 512
 ORDER = [0, 1, 2, 3]
 BLOCK = 256
 BLOCKS = 4
+FILLER = 64
 
 
 def weave_words(copy, woven, pairs):
@@ -174,20 +175,17 @@ def tile_attend_ghub_pl_sgd_kernel(tc, xT, wT, y, wt, xm, offs, out_0, out_1, ou
                 for t in range(2 * u, 2 * u + 2):
                     weigh_targets(h, t)
 
-        decayed.append(pool.tile([P, N], F32, name="y_pair1"))
-        for h in range(2):
-            nc.scalar.activation(decayed[LANES - 1][:, halves[h]], picked_halves[h][:], COPY, scale=keep)
-
         shared = pool.tile([P, 7 * H], BF16, name="shared", align_bytes=64)
-        xm16 = [shared[:, 3 * H : 7 * H], shared[:, 0 : 4 * H]]
+        xm16 = [shared[:, 3 * H : 7 * H], pool.tile([P, 4 * H], BF16, name="xm16_1", align_bytes=64)[:]]
 
-        def deal_xm(u):
-            nc.scalar.copy(
-                out=xm16[u].rearrange("p (e s j) -> p s j e", e=2, j=LANES),
-                in_=xm_raw[:].rearrange("p j (s u e) -> p u s j e", u=2, e=2)[:, u],
+        def deal_xm(copy, u, lo, hi):
+            copy(
+                out=xm16[u].rearrange("p (e s j) -> p s j e", e=2, j=LANES)[:, lo:hi],
+                in_=xm_raw[:].rearrange("p j (s u e) -> p u s j e", u=2, e=2)[:, u, lo:hi],
             )
 
-        deal_xm(0)
+        deal_xm(nc.scalar.copy, 0, 0, P // 2)
+        deal_xm(nc.scalar.copy, 1, 0, P)
 
         g_rows = [
             pool.tile([P, 1, LANES, H], BF16, name="g_rows0"),
@@ -282,19 +280,24 @@ def tile_attend_ghub_pl_sgd_kernel(tc, xT, wT, y, wt, xm, offs, out_0, out_1, ou
         subtract_targets(1, 3)
         for t in range(LANES - 1):
             clamp(1, t)
+        deal_xm(nc.vector.tensor_copy, 0, P // 2, P)
         quantize_xm(0, 1)
         early_bank = gradient(ORDER[0], "bank0", 0)
         quantize_xm(1, 1)
         quarters = [(0, H // 2), (H // 2, H)]
         for lo, hi in quarters:
             clamp(1, LANES - 1, lo, hi)
-        weave_g(nc.scalar.copy, 1, *pieces[1])
+        weave_g(nc.vector.tensor_copy, 1, *pieces[1])
         weave_g(nc.vector.tensor_copy, 2, *pieces[2])
-        early_step = pool.tile([P, H], F32, name="residual1_3", align_bytes=64)
-        nc.scalar.activation(early_step[:], early_bank[:, halves[1]], COPY, scale=-LR)
-        deal_xm(1)
-        quantize_g(2)
+        early_step = shared[:, 0 : 2 * H].bitcast(F32)
+        nc.scalar.activation(early_step, early_bank[:, halves[1]], COPY, scale=-LR)
         quantize_g(1)
+        quantize_xm(2, 2)
+        quantize_g(2)
+
+        decayed.append(pool.tile([P, N], F32, name="g16_%d" % pieces[2][0], align_bytes=64))
+        for h in range(2):
+            nc.scalar.activation(decayed[LANES - 1][:, halves[h]], picked_halves[h][:], COPY, scale=keep)
 
         steps = []
 
@@ -306,10 +309,14 @@ def tile_attend_ghub_pl_sgd_kernel(tc, xT, wT, y, wt, xm, offs, out_0, out_1, ou
             listed = offsets[:, slots.start // 16 : slots.stop // 16]
             nc.vector.tensor_tensor(table[t][:].indirect(listed), kept, step, ALU.add)
 
-        take_step(0, gradient(0, "bank1"), H, "step0")
-        take_step(1, gradient(1, "bank2"), 0, "step1")
-        scatter(0, halves[0], decayed[0][:, halves[0]], early_step[:])
-        quantize_xm(2, 2)
+        second_bank = gradient(1, "bank2")
+        first_bank = gradient(0, "bank1")
+        filler_step = pool.tile([P, FILLER], F32, name="filler_step")
+        nc.scalar.activation(filler_step[:], second_bank[:, 0:FILLER], COPY, scale=-LR)
+        take_step(0, first_bank, H, "step0")
+        take_step(1, second_bank, FILLER, "xm_scales0")
+        scatter(0, halves[0], decayed[0][:, halves[0]], early_step)
+        scatter(1, slice(0, FILLER), decayed[1][:, 0:FILLER], filler_step[:])
         for t in range(2, LANES):
             take_step(t, gradient(t, "bank%d" % (t + 1)), 0, "step%d" % t)
 
@@ -329,7 +336,7 @@ def tile_attend_ghub_pl_sgd_kernel(tc, xT, wT, y, wt, xm, offs, out_0, out_1, ou
             )
 
         for t in ORDER:
-            slots = halves[1] if t == 0 else slice(0, N)
+            slots = slice({0: H, 1: FILLER}.get(t, 0), N)
             scatter(t, slots, decayed[t][:, slots], steps[t][:, slots])
             nc.sync.dma_start(out=out_rows[:, t, :], in_=table[t][:])
             if t != ORDER[-1]:
@@ -364,7 +371,8 @@ def tile_attend_ghub_pl_sgd_kernel(tc, xT, wT, y, wt, xm, offs, out_0, out_1, ou
         last = ORDER[-1]
         round_rows(nc.vector.tensor_copy, last, 0, 1)
         round_rows(nc.vector.tensor_copy, last, 1, 2)
-        round_rows(nc.scalar.copy, last, 2, 4)
+        round_rows(nc.vector.tensor_copy, last, 2, 3)
+        round_rows(nc.scalar.copy, last, 3, 4)
         round_pairs(last, 0, 2)
         round_pairs(last, 2, 3)
         weave(3)

@@ -19,9 +19,9 @@ COPY = mybir.ActivationFunctionType.Copy
 
 P = 128
 LANES = 4
+LAST = LANES - 1
 H = N // 2
-PASS = 512
-ORDER = [0, 1, 2, 3]
+PASS = P * LANES
 BLOCK = 256
 BLOCKS = 4
 FILLER = 64
@@ -68,17 +68,15 @@ def tile_attend_ghub_pl_sgd_kernel(tc, xT, wT, y, wt, xm, offs, out_0, out_1, ou
 
         nc.sync.dma_start(out=source[0][:], in_=w_rows[:, 0, :])
         nc.sync.dma_start(offsets[:], offs)
-        nc.sync.dma_start(out=source[1][:], in_=w_rows[:, 1, :])
-        for t in range(2, LANES):
+        for t in range(1, LANES):
             nc.sync.dma_start(out=source[t][:], in_=w_rows[:, t, :])
         nc.sync.dma_start(out=x_raw[:], in_=x_rows)
         nc.sync.dma_start(out=weights[:], in_=wt_rows)
         for u in range(2):
             nc.sync.dma_start(out=y_pairs[u][:], in_=y_rows[:, 2 * u : 2 * u + 2, :])
         nc.sync.dma_start(out=xm_raw[:], in_=xm_rows)
-        for t in ORDER[1:]:
+        for t in range(1, LANES):
             nc.sync.dma_start(out=table[t][:], in_=w_rows[:, t, :])
-
 
         g_codes = pool.tile([P, H + N], U32, name="g_codes", align_bytes=64)
         g_scales = pool.tile([P, H + N], U8, name="g_scales", align_bytes=64)
@@ -87,9 +85,9 @@ def tile_attend_ghub_pl_sgd_kernel(tc, xT, wT, y, wt, xm, offs, out_0, out_1, ou
 
         halves = [slice(0, H), slice(H, N)]
         w16 = [pool.tile([P, H, LANES], BF16, name="w16_%d" % h, align_bytes=64) for h in range(2)]
-        decayed = [pool.tile([P, N], F32, name="decayed%d" % t) for t in range(LANES - 1)]
+        decayed = [pool.tile([P, N], F32, name="decayed%d" % t) for t in range(LAST)]
         keep = 1.0 - LR * WD
-        picked = [pool.tile([P, N], F32, name="picked%d" % t) for t in range(LANES - 1)]
+        picked = [pool.tile([P, N], F32, name="picked%d" % t) for t in range(LAST)]
 
         def round_shared(t, sources):
             for h in range(2):
@@ -98,7 +96,7 @@ def tile_attend_ghub_pl_sgd_kernel(tc, xT, wT, y, wt, xm, offs, out_0, out_1, ou
                     quarter = slice(q * H // 2, (q + 1) * H // 2)
                     copy(out=w16[h][:, quarter, t], in_=sources[h][:, quarter])
 
-        for t in range(LANES - 1):
+        for t in range(LAST):
             nc.vector.tensor_copy(picked[t][:], source[t][:].indirect(offsets[:]))
             if t < 2:
                 for h in range(2):
@@ -109,12 +107,11 @@ def tile_attend_ghub_pl_sgd_kernel(tc, xT, wT, y, wt, xm, offs, out_0, out_1, ou
             else:
                 round_shared(t, [picked[t][:, half] for half in halves])
                 nc.scalar.activation(decayed[t][:], picked[t][:], COPY, scale=keep)
-        t = LANES - 1
         picked_halves = [pool.tile([P, H], F32, name="picked_half%d" % h) for h in range(2)]
         for h in range(2):
             listed = offsets[:, h * H // 16 : (h + 1) * H // 16]
-            nc.vector.tensor_copy(picked_halves[h][:], source[t][:].indirect(listed))
-        round_shared(t, picked_halves)
+            nc.vector.tensor_copy(picked_halves[h][:], source[LAST][:].indirect(listed))
+        round_shared(LAST, picked_halves)
 
         w_codes = [pool.tile([P, H], U32, name="w_codes0", align_bytes=64)]
         w_scales = [pool.tile([P, H], U8, name="w_scales%d" % h, align_bytes=64) for h in range(2)]
@@ -135,8 +132,8 @@ def tile_attend_ghub_pl_sgd_kernel(tc, xT, wT, y, wt, xm, offs, out_0, out_1, ou
         ]
         weighted_y = [pool.tile([P, LANES, H], F32, name="weighted_y%d" % h) for h in range(2)]
 
-        def deal_x(copy, u, lo, hi):
-            copy(out=x16[u][:, :, lo:hi].rearrange("p e s j -> p s j e"), in_=x_by_pair[:, u, lo:hi])
+        def deal_x(copy, u):
+            copy(out=x16[u][:].rearrange("p e s j -> p s j e"), in_=x_by_pair[:, u])
 
         def quantize_x(t):
             nc.vector.quantize_mx(
@@ -159,8 +156,8 @@ def tile_attend_ghub_pl_sgd_kernel(tc, xT, wT, y, wt, xm, offs, out_0, out_1, ou
         def weigh_targets(h, t):
             nc.scalar.activation(weighted_y[h][:, t, :], y_raw[t][:, halves[h]], COPY, scale=weight[t])
 
-        deal_x(nc.vector.tensor_copy, 0, 0, P)
-        deal_x(nc.scalar.copy, 1, 0, P)
+        deal_x(nc.vector.tensor_copy, 0)
+        deal_x(nc.scalar.copy, 1)
         upper = pool.tile([P, LANES], F32, name="upper")
         lower = pool.tile([P, LANES], F32, name="lower")
         nc.vector.scalar_tensor_tensor(upper[:], weights[:], -1.0, weights[:], ALU.mult, ALU.max)
@@ -178,18 +175,15 @@ def tile_attend_ghub_pl_sgd_kernel(tc, xT, wT, y, wt, xm, offs, out_0, out_1, ou
         shared = pool.tile([P, 7 * H], BF16, name="shared", align_bytes=64)
         xm16 = [shared[:, 3 * H : 7 * H], pool.tile([P, 4 * H], BF16, name="xm16_1", align_bytes=64)[:]]
 
-        def deal_xm(copy, u, lo, hi):
-            copy(
-                out=xm16[u].rearrange("p (e s j) -> p s j e", e=2, j=LANES)[:, lo:hi],
-                in_=xm_raw[:].rearrange("p j (s u e) -> p u s j e", u=2, e=2)[:, u, lo:hi],
+        for u in range(2):
+            nc.scalar.copy(
+                out=xm16[u].rearrange("p (e s j) -> p s j e", e=2, j=LANES),
+                in_=xm_raw[:].rearrange("p j (s u e) -> p u s j e", u=2, e=2)[:, u],
             )
 
-        deal_xm(nc.scalar.copy, 0, 0, P // 2)
-        deal_xm(nc.scalar.copy, 1, 0, P)
-
         g_rows = [
-            pool.tile([P, 1, LANES, H], BF16, name="g_rows0"),
-            shared[:, 0 : 4 * H].rearrange("p (o t c) -> p o t c", o=1, t=LANES),
+            pool.tile([P, LANES, H], BF16, name="g_rows0"),
+            shared[:, 0 : 4 * H].rearrange("p (t c) -> p t c", t=LANES),
         ]
         pieces = [(0, H), (H, H + H // 2), (H + H // 2, N)]
         g16 = [pool.tile([P, hi - lo, LANES], BF16, name="g16_%d" % lo, align_bytes=64) for lo, hi in pieces]
@@ -212,7 +206,7 @@ def tile_attend_ghub_pl_sgd_kernel(tc, xT, wT, y, wt, xm, offs, out_0, out_1, ou
 
         def clamp(h, t, lo=0, hi=H):
             nc.vector.tensor_scalar(
-                g_rows[h][:, 0, t, lo:hi],
+                g_rows[h][:, t, lo:hi],
                 residual[h][t][:, lo:hi],
                 lower[:, t : t + 1],
                 upper[:, t : t + 1],
@@ -220,12 +214,12 @@ def tile_attend_ghub_pl_sgd_kernel(tc, xT, wT, y, wt, xm, offs, out_0, out_1, ou
                 ALU.min,
             )
 
-        def weave_g(copy, k, lo, hi):
-            first = pieces[k][0]
+        def weave_g(k):
+            lo, hi = pieces[k]
             h = lo // H
-            copy(
-                out=g16[k][:, lo - first : hi - first].rearrange("p (c i) t -> p c t i", i=4),
-                in_=g_rows[h][:, 0, :, lo - h * H : hi - h * H].rearrange("p t (c i) -> p c t i", i=4),
+            nc.vector.tensor_copy(
+                out=g16[k][:].rearrange("p (c i) t -> p c t i", i=4),
+                in_=g_rows[h][:, :, lo - h * H : hi - h * H].rearrange("p t (c i) -> p c t i", i=4),
             )
 
         def quantize_g(k):
@@ -272,32 +266,31 @@ def tile_attend_ghub_pl_sgd_kernel(tc, xT, wT, y, wt, xm, offs, out_0, out_1, ou
             subtract_targets(0, t)
             clamp(0, t - 1)
         subtract_targets(1, 0)
-        clamp(0, LANES - 1)
+        clamp(0, LAST)
         subtract_targets(1, 1)
-        weave_g(nc.vector.tensor_copy, 0, 0, H)
+        weave_g(0)
         subtract_targets(1, 2)
         quantize_g(0)
         subtract_targets(1, 3)
-        for t in range(LANES - 1):
+        for t in range(LAST):
             clamp(1, t)
-        deal_xm(nc.vector.tensor_copy, 0, P // 2, P)
         quantize_xm(0, 1)
-        early_bank = gradient(ORDER[0], "bank0", 0)
+        early_bank = gradient(0, "bank0", 0)
         quantize_xm(1, 1)
-        quarters = [(0, H // 2), (H // 2, H)]
-        for lo, hi in quarters:
-            clamp(1, LANES - 1, lo, hi)
-        weave_g(nc.vector.tensor_copy, 1, *pieces[1])
-        weave_g(nc.vector.tensor_copy, 2, *pieces[2])
-        early_step = shared[:, 0 : 2 * H].bitcast(F32)
-        nc.scalar.activation(early_step, early_bank[:, halves[1]], COPY, scale=-LR)
+        filler_bank = gradient(1, "bank5", 0)
+        for lo, hi in pieces[1:]:
+            clamp(1, LAST, lo - H, hi - H)
+        weave_g(1)
+        weave_g(2)
+        early_step = pool.tile([P, H], F32, name="residual1_3", align_bytes=64)
+        nc.scalar.activation(early_step[:], early_bank[:, halves[1]], COPY, scale=-LR)
         quantize_g(1)
         quantize_xm(2, 2)
         quantize_g(2)
 
-        decayed.append(pool.tile([P, N], F32, name="g16_%d" % pieces[2][0], align_bytes=64))
+        decayed.append(pool.tile([P, N], F32, name="g16_%d" % pieces[1][0], align_bytes=64))
         for h in range(2):
-            nc.scalar.activation(decayed[LANES - 1][:, halves[h]], picked_halves[h][:], COPY, scale=keep)
+            nc.scalar.activation(decayed[LAST][:, halves[h]], picked_halves[h][:], COPY, scale=keep)
 
         steps = []
 
@@ -309,13 +302,11 @@ def tile_attend_ghub_pl_sgd_kernel(tc, xT, wT, y, wt, xm, offs, out_0, out_1, ou
             listed = offsets[:, slots.start // 16 : slots.stop // 16]
             nc.vector.tensor_tensor(table[t][:].indirect(listed), kept, step, ALU.add)
 
-        second_bank = gradient(1, "bank2")
-        first_bank = gradient(0, "bank1")
-        filler_step = pool.tile([P, FILLER], F32, name="filler_step")
-        nc.scalar.activation(filler_step[:], second_bank[:, 0:FILLER], COPY, scale=-LR)
-        take_step(0, first_bank, H, "step0")
-        take_step(1, second_bank, FILLER, "xm_scales0")
-        scatter(0, halves[0], decayed[0][:, halves[0]], early_step)
+        filler_step = pool.tile([P, FILLER], F32, name="g16_%d" % pieces[2][0], align_bytes=64)
+        nc.scalar.activation(filler_step[:], filler_bank[:, H : H + FILLER], COPY, scale=-LR)
+        take_step(0, gradient(0, "bank1"), H, "step0")
+        take_step(1, gradient(1, "bank2"), FILLER, "step1")
+        scatter(0, halves[0], decayed[0][:, halves[0]], early_step[:])
         scatter(1, slice(0, FILLER), decayed[1][:, 0:FILLER], filler_step[:])
         for t in range(2, LANES):
             take_step(t, gradient(t, "bank%d" % (t + 1)), 0, "step%d" % t)
@@ -335,11 +326,11 @@ def tile_attend_ghub_pl_sgd_kernel(tc, xT, wT, y, wt, xm, offs, out_0, out_1, ou
                 in_=table[t][:, (BLOCKS + lo) * BLOCK : (BLOCKS + hi) * BLOCK].rearrange("p (k c) -> p k c", c=BLOCK),
             )
 
-        for t in ORDER:
-            slots = slice({0: H, 1: FILLER}.get(t, 0), N)
+        for t, done in enumerate([H, FILLER, 0, 0]):
+            slots = slice(done, N)
             scatter(t, slots, decayed[t][:, slots], steps[t][:, slots])
             nc.sync.dma_start(out=out_rows[:, t, :], in_=table[t][:])
-            if t != ORDER[-1]:
+            if t != LAST:
                 round_pairs(t, 0, BLOCKS)
                 round_rows(nc.scalar.copy, t, 0, BLOCKS)
 
@@ -356,35 +347,40 @@ def tile_attend_ghub_pl_sgd_kernel(tc, xT, wT, y, wt, xm, offs, out_0, out_1, ou
             else:
                 weave_words(nc.scalar.copy, woven[c][:], pairs[:, lo - BLOCKS : hi - BLOCKS])
 
-        def quantize_out(c):
-            first, stop = chunks[c]
-            codes = pool.tile([P, (stop - first) * BLOCK], U32, name="out_codes%d" % c, align_bytes=64)
-            for k in range(first, stop):
-                here = slice((k - first) * BLOCK, (k - first + 1) * BLOCK)
+        woven_block = [
+            woven[c][:, (k - lo) * BLOCK : (k - lo + 1) * BLOCK] for c, (lo, hi) in enumerate(chunks) for k in range(lo, hi)
+        ]
+
+        def quantize_out(g):
+            codes = pool.tile([P, 2 * BLOCK], U32, name="out_codes%d" % g, align_bytes=64)
+            for half in range(2):
+                here = slice(half * BLOCK, (half + 1) * BLOCK)
                 nc.vector.quantize_mx(
                     out=codes[:, here].bitcast(E4M3),
-                    scales=out_scales[4 * (k // 2) : P, (k % 2) * BLOCK : (k % 2 + 1) * BLOCK],
-                    in_=woven[c][:, here].rearrange("p c l -> p (c l)"),
+                    scales=out_scales[4 * g : P, here],
+                    in_=woven_block[2 * g + half].rearrange("p c l -> p (c l)"),
                 )
-            nc.sync.dma_start(out=words_out[:, first * BLOCK : stop * BLOCK], in_=codes[:].bitcast(I32))
+            runs = [(0, BLOCK), (BLOCK, 2 * BLOCK)] if g == 3 else [(0, 2 * BLOCK)]
+            for lo, hi in runs:
+                nc.sync.dma_start(
+                    out=words_out[:, 2 * g * BLOCK + lo : 2 * g * BLOCK + hi], in_=codes[:, lo:hi].bitcast(I32)
+                )
 
-        last = ORDER[-1]
-        round_rows(nc.vector.tensor_copy, last, 0, 1)
-        round_rows(nc.vector.tensor_copy, last, 1, 2)
-        round_rows(nc.vector.tensor_copy, last, 2, 3)
-        round_rows(nc.scalar.copy, last, 3, 4)
-        round_pairs(last, 0, 2)
-        round_pairs(last, 2, 3)
+        for k in range(BLOCKS - 1):
+            round_rows(nc.vector.tensor_copy, LAST, k, k + 1)
+        round_rows(nc.scalar.copy, LAST, BLOCKS - 1, BLOCKS)
+        round_pairs(LAST, 0, 2)
+        round_pairs(LAST, 2, 3)
         weave(3)
-        round_pairs(last, 3, 4)
+        round_pairs(LAST, 3, 4)
         weave(4)
         weave(5)
         weave(0)
         weave(1)
         quantize_out(0)
         weave(2)
-        for c in range(1, len(chunks)):
-            quantize_out(c)
+        for g in (2, 1, 3):
+            quantize_out(g)
         for q in range(4):
             queue = nc.scalar if q % 2 else nc.sync
             queue.dma_start(

@@ -23,21 +23,14 @@ LAST = LANES - 1
 H = N // 2
 PASS = P * LANES
 BLOCK = 256
-BLOCKS = 4
-FILLER = 64
+BLOCKS = T // BLOCK
+SCALAR_BLOCKS = 4
 
 
 def weave_words(copy, woven, pairs):
     copy(
         out=woven.rearrange("p c l -> p (c l)").bitcast(F32).rearrange("p (k c h) -> p k c h", c=BLOCK, h=2),
         in_=pairs.rearrange("p k h c e -> p k h (c e)").bitcast(F32).rearrange("p k h c -> p k c h"),
-    )
-
-
-def weave_rows(copy, woven, rows):
-    copy(
-        out=woven.rearrange("p (k c i) t -> p k c t i", c=BLOCK // 4, i=4),
-        in_=rows.rearrange("p k t (c i) -> p k c t i", i=4),
     )
 
 
@@ -75,19 +68,17 @@ def tile_attend_ghub_pl_sgd_kernel(tc, xT, wT, y, wt, xm, offs, out_0, out_1, ou
         for u in range(2):
             nc.sync.dma_start(out=y_pairs[u][:], in_=y_rows[:, 2 * u : 2 * u + 2, :])
         nc.sync.dma_start(out=xm_raw[:], in_=xm_rows)
-        for t in range(1, LANES):
-            nc.sync.dma_start(out=table[t][:], in_=w_rows[:, t, :])
+        nc.sync.dma_start(out=table[LAST][:], in_=w_rows[:, LAST, :])
 
-        g_codes = pool.tile([P, H + N], U32, name="g_codes", align_bytes=64)
-        g_scales = pool.tile([P, H + N], U8, name="g_scales", align_bytes=64)
-        nc.vector.memset(g_codes[:, 0:H], 0)
-        nc.vector.memset(g_scales[:, 0:H].bitcast(U32), 0)
+        g_codes = pool.tile([P, N], U32, name="g_codes", align_bytes=64)
+        g_scales = pool.tile([P, N], U8, name="g_scales", align_bytes=64)
 
         halves = [slice(0, H), slice(H, N)]
         w16 = [pool.tile([P, H, LANES], BF16, name="w16_%d" % h, align_bytes=64) for h in range(2)]
-        decayed = [pool.tile([P, N], F32, name="decayed%d" % t) for t in range(LAST)]
         keep = 1.0 - LR * WD
-        picked = [pool.tile([P, N], F32, name="picked%d" % t) for t in range(LAST)]
+        picked_pairs = [pool.tile([P, 2, N], F32, name="picked%d" % u) for u in range(2)]
+        picked = [picked_pairs[t // 2][:, t % 2, :] for t in range(LANES)]
+        decayed = {t: pool.tile([P, H], F32, name="decayed%d" % t) for t in (0, LAST)}
 
         def round_shared(t, sources):
             for h in range(2):
@@ -96,21 +87,29 @@ def tile_attend_ghub_pl_sgd_kernel(tc, xT, wT, y, wt, xm, offs, out_0, out_1, ou
                     quarter = slice(q * H // 2, (q + 1) * H // 2)
                     copy(out=w16[h][:, quarter, t], in_=sources[h][:, quarter])
 
-        for t in range(LAST):
-            nc.vector.tensor_copy(picked[t][:], source[t][:].indirect(offsets[:]))
+        def scalar_move(out, in_):
+            nc.scalar.activation(out, in_, COPY)
+
+        def copy_table(copy, t, lo, hi):
+            columns = slice(lo * T // 4, hi * T // 4)
+            copy(out=table[t][:, columns], in_=source[t][:, columns])
+
+        for t, scalar_quarters in enumerate([2, 1, 2]):
+            copy_table(scalar_move, t, 0, min(scalar_quarters, 2 - t // 2))
+            nc.vector.tensor_copy(picked[t], source[t][:].indirect(offsets[:]))
             if t < 2:
                 for h in range(2):
                     nc.scalar.copy(out=w16[h][:, :, t], in_=picked[t][:, halves[h]])
-                nc.vector.tensor_scalar(decayed[t][:], picked[t][:], keep, None, ALU.mult)
-                columns = slice(t * T // 2, (t + 1) * T // 2)
-                nc.vector.tensor_copy(table[0][:, columns], source[0][:, columns])
+                if t == 0:
+                    nc.vector.tensor_scalar(decayed[t][:], picked[t][:, halves[1]], keep, None, ALU.mult)
             else:
                 round_shared(t, [picked[t][:, half] for half in halves])
-                nc.scalar.activation(decayed[t][:], picked[t][:], COPY, scale=keep)
-        picked_halves = [pool.tile([P, H], F32, name="picked_half%d" % h) for h in range(2)]
+                copy_table(scalar_move, t, 1, 2)
+            copy_table(nc.vector.tensor_copy, t, scalar_quarters, 4)
+        picked_halves = [picked[LAST][:, half] for half in halves]
         for h in range(2):
             listed = offsets[:, h * H // 16 : (h + 1) * H // 16]
-            nc.vector.tensor_copy(picked_halves[h][:], source[LAST][:].indirect(listed))
+            nc.vector.tensor_copy(picked_halves[h], source[LAST][:].indirect(listed))
         round_shared(LAST, picked_halves)
 
         w_codes = [pool.tile([P, H], U32, name="w_codes0", align_bytes=64)]
@@ -172,8 +171,9 @@ def tile_attend_ghub_pl_sgd_kernel(tc, xT, wT, y, wt, xm, offs, out_0, out_1, ou
                 for t in range(2 * u, 2 * u + 2):
                     weigh_targets(h, t)
 
-        shared = pool.tile([P, 7 * H], BF16, name="shared", align_bytes=64)
-        xm16 = [shared[:, 3 * H : 7 * H], pool.tile([P, 4 * H], BF16, name="xm16_1", align_bytes=64)[:]]
+        nc.scalar.activation(decayed[LAST][:], picked_halves[0], COPY, scale=keep)
+        shared = pool.tile([P, 4 * H], BF16, name="shared", align_bytes=64)
+        xm16 = [shared[:], pool.tile([P, 4 * H], BF16, name="xm16_1", align_bytes=64)[:]]
 
         for u in range(2):
             nc.scalar.copy(
@@ -186,7 +186,7 @@ def tile_attend_ghub_pl_sgd_kernel(tc, xT, wT, y, wt, xm, offs, out_0, out_1, ou
             shared[:, 0 : 4 * H].rearrange("p (t c) -> p t c", t=LANES),
         ]
         pieces = [(0, H), (H, H + H // 2), (H + H // 2, N)]
-        g16 = [pool.tile([P, hi - lo, LANES], BF16, name="g16_%d" % lo, align_bytes=64) for lo, hi in pieces]
+        g16 = []
         residual = [
             [pool.tile([P, H], F32, name="residual%d_%d" % (h, t), align_bytes=64) for t in range(LANES)]
             for h in range(2)
@@ -217,6 +217,8 @@ def tile_attend_ghub_pl_sgd_kernel(tc, xT, wT, y, wt, xm, offs, out_0, out_1, ou
         def weave_g(k):
             lo, hi = pieces[k]
             h = lo // H
+            name = "g16_%d" % k
+            g16.append(pool.tile([P, hi - lo, LANES], BF16, name=name, align_bytes=64))
             nc.vector.tensor_copy(
                 out=g16[k][:].rearrange("p (c i) t -> p c t i", i=4),
                 in_=g_rows[h][:, :, lo - h * H : hi - h * H].rearrange("p t (c i) -> p c t i", i=4),
@@ -225,8 +227,8 @@ def tile_attend_ghub_pl_sgd_kernel(tc, xT, wT, y, wt, xm, offs, out_0, out_1, ou
         def quantize_g(k):
             lo, hi = pieces[k]
             nc.vector.quantize_mx(
-                out=g_codes[:, H + lo : H + hi].bitcast(E5M2),
-                scales=g_scales[:, H + lo : H + hi],
+                out=g_codes[:, lo:hi].bitcast(E5M2),
+                scales=g_scales[:, lo:hi],
                 in_=g16[k][:].rearrange("p i t -> p (i t)"),
             )
 
@@ -241,18 +243,34 @@ def tile_attend_ghub_pl_sgd_kernel(tc, xT, wT, y, wt, xm, offs, out_0, out_1, ou
                 xm_codes.append(codes[:, e * P : (e + 1) * P])
                 xm_scales.append(scales[:, e * P : (e + 1) * P])
 
-        def gradient(t, name, first=H):
-            bank = psum.tile([P, N], F32, name=name)
+        fresh = {}
+
+        def update(t, first, count, bank_number, on_vector=False):
+            slots = slice(first * H, (first + count) * H)
+            bank = psum.tile([P, count * H], F32, name="bank%d" % bank_number)
             nc.tensor.matmul_mx(
                 out=bank[:],
                 lhsT=xm_codes[t].bitcast(E4M3),
                 lhsT_scale=xm_scales[t],
-                rhs=g_codes[:, first : first + N].bitcast(E5M2),
-                rhs_scale=g_scales[:, first : first + N],
+                rhs=g_codes[:, slots].bitcast(E5M2),
+                rhs_scale=g_scales[:, slots],
                 start=True,
                 stop=True,
             )
-            return bank
+            values = pool.tile([P, count * H], F32, name="fresh%d_%d" % (t, first))
+            if on_vector:
+                nc.vector.scalar_tensor_tensor(values[:], bank[:], -LR, decayed[t][:], ALU.mult, ALU.add)
+            else:
+                nc.vector.scalar_tensor_tensor(values[:], bank[:], -LR / keep, picked[t][:, slots], ALU.mult, ALU.add)
+            for e in range(count):
+                fresh[t, first + e] = values[:, e * H : (e + 1) * H]
+
+        def scatter(t, h, on_vector):
+            window = table[t][:].indirect(offsets[:, h * H // 16 : (h + 1) * H // 16])
+            if on_vector:
+                nc.vector.tensor_copy(window, fresh[t, h])
+            else:
+                nc.scalar.activation(window, fresh[t, h], COPY, scale=keep)
 
         subtract_targets(0, 0)
         subtract_targets(0, 1)
@@ -272,118 +290,94 @@ def tile_attend_ghub_pl_sgd_kernel(tc, xT, wT, y, wt, xm, offs, out_0, out_1, ou
         subtract_targets(1, 2)
         quantize_g(0)
         subtract_targets(1, 3)
-        for t in range(LAST):
-            clamp(1, t)
         quantize_xm(0, 1)
-        early_bank = gradient(0, "bank0", 0)
         quantize_xm(1, 1)
-        filler_bank = gradient(1, "bank5", 0)
+        clamp(1, 0)
+        clamp(1, 1)
+        update(0, 0, 1, 0)
+        scatter(0, 0, False)
+        clamp(1, 2)
         for lo, hi in pieces[1:]:
             clamp(1, LAST, lo - H, hi - H)
         weave_g(1)
+        update(1, 0, 1, 1)
+        scatter(1, 0, False)
         weave_g(2)
-        early_step = pool.tile([P, H], F32, name="residual1_3", align_bytes=64)
-        nc.scalar.activation(early_step[:], early_bank[:, halves[1]], COPY, scale=-LR)
         quantize_g(1)
         quantize_xm(2, 2)
         quantize_g(2)
+        update(2, 0, 1, 2)
+        scatter(2, 0, False)
+        update(0, 1, 1, 4, True)
+        update(1, 1, 1, 5)
 
-        decayed.append(pool.tile([P, N], F32, name="g16_%d" % pieces[1][0], align_bytes=64))
-        for h in range(2):
-            nc.scalar.activation(decayed[LAST][:, halves[h]], picked_halves[h][:], COPY, scale=keep)
 
-        steps = []
-
-        def take_step(t, bank, first, name):
-            steps.append(pool.tile([P, N], F32, name=name, align_bytes=64))
-            nc.scalar.activation(steps[t][:, first:N], bank[:, first:N], COPY, scale=-LR)
-
-        def scatter(t, slots, kept, step):
-            listed = offsets[:, slots.start // 16 : slots.stop // 16]
-            nc.vector.tensor_tensor(table[t][:].indirect(listed), kept, step, ALU.add)
-
-        filler_step = pool.tile([P, FILLER], F32, name="g16_%d" % pieces[2][0], align_bytes=64)
-        nc.scalar.activation(filler_step[:], filler_bank[:, H : H + FILLER], COPY, scale=-LR)
-        take_step(0, gradient(0, "bank1"), H, "step0")
-        take_step(1, gradient(1, "bank2"), FILLER, "step1")
-        scatter(0, halves[0], decayed[0][:, halves[0]], early_step[:])
-        scatter(1, slice(0, FILLER), decayed[1][:, 0:FILLER], filler_step[:])
-        for t in range(2, LANES):
-            take_step(t, gradient(t, "bank%d" % (t + 1)), 0, "step%d" % t)
-
-        rows = pool.tile([P, BLOCKS, LANES, BLOCK], BF16, name="rows")
-        pairs = pool.tile([P, BLOCKS, 2, BLOCK, 2], BF16, name="pairs")
-
-        def round_rows(copy, t, lo, hi):
+        def round_pairs(copy, t, lo, hi):
             copy(
-                out=rows[:, lo:hi, t, :],
+                out=pairs[:, lo:hi, t // 2, :, t % 2],
                 in_=table[t][:, lo * BLOCK : hi * BLOCK].rearrange("p (k c) -> p k c", c=BLOCK),
             )
 
-        def round_pairs(t, lo, hi):
-            nc.scalar.copy(
-                out=pairs[:, lo:hi, t // 2, :, t % 2],
-                in_=table[t][:, (BLOCKS + lo) * BLOCK : (BLOCKS + hi) * BLOCK].rearrange("p (k c) -> p k c", c=BLOCK),
-            )
-
-        for t, done in enumerate([H, FILLER, 0, 0]):
-            slots = slice(done, N)
-            scatter(t, slots, decayed[t][:, slots], steps[t][:, slots])
+        def store(t):
             nc.sync.dma_start(out=out_rows[:, t, :], in_=table[t][:])
-            if t != LAST:
-                round_pairs(t, 0, BLOCKS)
-                round_rows(nc.scalar.copy, t, 0, BLOCKS)
+
+        scatter(0, 1, True)
+        store(0)
+        scatter(1, 1, False)
+        store(1)
+        update(3, 0, 1, 3, True)
+        update(2, 1, 1, 6)
+        update(3, 1, 1, 7)
+        scatter(3, 0, True)
+        scatter(2, 1, False)
+        store(2)
+        scatter(3, 1, False)
+        store(3)
+        split = BLOCKS - SCALAR_BLOCKS
+        pairs = pool.tile([P, BLOCKS, 2, BLOCK, 2], BF16, name="picked1")
+        round_pairs(nc.vector.tensor_copy, 0, 0, BLOCKS)
+        round_pairs(nc.vector.tensor_copy, 1, 0, BLOCKS)
+        round_pairs(nc.vector.tensor_copy, 2, 0, split)
 
         out_scales = pool.tile([P, T // 4], U8, name="out_scales", align_bytes=64)
-        chunks = [(0, 1), (1, 2), (2, 4), (4, 6), (6, 7), (7, 8)]
-        woven = [
-            pool.tile([P, (hi - lo) * BLOCK, LANES], BF16, name="woven%d" % lo, align_bytes=64) for lo, hi in chunks
-        ]
+        woven = [pool.tile([P, BLOCK, LANES], BF16, name="woven%d" % k, align_bytes=64) for k in range(BLOCKS)]
+        woven_block = [w[:] for w in woven]
 
-        def weave(c):
-            lo, hi = chunks[c]
-            if lo < BLOCKS:
-                weave_rows(nc.vector.tensor_copy, woven[c][:], rows[:, lo:hi])
-            else:
-                weave_words(nc.scalar.copy, woven[c][:], pairs[:, lo - BLOCKS : hi - BLOCKS])
+        def weave(copy, k):
+            weave_words(copy, woven[k][:], pairs[:, k : k + 1])
 
-        woven_block = [
-            woven[c][:, (k - lo) * BLOCK : (k - lo + 1) * BLOCK] for c, (lo, hi) in enumerate(chunks) for k in range(lo, hi)
-        ]
+        codes = pool.tile([P, T], U32, name="out_codes", align_bytes=64)
 
-        def quantize_out(g):
-            codes = pool.tile([P, 2 * BLOCK], U32, name="out_codes%d" % g, align_bytes=64)
-            for half in range(2):
-                here = slice(half * BLOCK, (half + 1) * BLOCK)
-                nc.vector.quantize_mx(
-                    out=codes[:, here].bitcast(E4M3),
-                    scales=out_scales[4 * g : P, here],
-                    in_=woven_block[2 * g + half].rearrange("p c l -> p (c l)"),
-                )
-            runs = [(0, BLOCK), (BLOCK, 2 * BLOCK)] if g == 3 else [(0, 2 * BLOCK)]
-            for lo, hi in runs:
-                nc.sync.dma_start(
-                    out=words_out[:, 2 * g * BLOCK + lo : 2 * g * BLOCK + hi], in_=codes[:, lo:hi].bitcast(I32)
-                )
+        def quantize_out(k):
+            here = slice(k % 2 * BLOCK, (k % 2 + 1) * BLOCK)
+            nc.vector.quantize_mx(
+                out=codes[:, k * BLOCK : (k + 1) * BLOCK].bitcast(E4M3),
+                scales=out_scales[4 * (k // 2) : P, here],
+                in_=woven_block[k].rearrange("p c l -> p (c l)"),
+            )
 
-        for k in range(BLOCKS - 1):
-            round_rows(nc.vector.tensor_copy, LAST, k, k + 1)
-        round_rows(nc.scalar.copy, LAST, BLOCKS - 1, BLOCKS)
-        round_pairs(LAST, 0, 2)
-        round_pairs(LAST, 2, 3)
-        weave(3)
-        round_pairs(LAST, 3, 4)
-        weave(4)
-        weave(5)
-        weave(0)
-        weave(1)
+        def store_words(lo, hi):
+            columns = slice(lo * BLOCK, hi * BLOCK)
+            nc.sync.dma_start(out=words_out[:, columns], in_=codes[:, columns].bitcast(I32))
+
+        for k in range(split, BLOCKS):
+            round_pairs(nc.scalar.copy, 2, k, k + 1)
+            round_pairs(nc.scalar.copy, 3, k, k + 1)
+            weave(nc.scalar.copy, k)
+        round_pairs(nc.vector.tensor_copy, 3, 0, 2)
+        round_pairs(nc.vector.tensor_copy, 3, 2, split)
+        weave(nc.vector.tensor_copy, 0)
+        weave(nc.vector.tensor_copy, 1)
+        weave(nc.vector.tensor_copy, 2)
         quantize_out(0)
-        weave(2)
-        for g in (2, 1, 3):
-            quantize_out(g)
+        quantize_out(1)
+        weave(nc.vector.tensor_copy, 3)
+        for lo, hi in [(0, 4), (4, 7), (7, 8)]:
+            for k in range(max(lo, 2), hi):
+                quantize_out(k)
+            store_words(lo, hi)
         for q in range(4):
-            queue = nc.scalar if q % 2 else nc.sync
-            queue.dma_start(
+            nc.sync.dma_start(
                 out=scales_out[4 * q : 4 * q + 4, :].rearrange("f (g w) -> g f w", g=4),
                 in_=out_scales[32 * q : 32 * q + 16, :].bitcast(I32),
             )

@@ -24,13 +24,16 @@ H = N // 2
 PASS = P * LANES
 BLOCK = 256
 BLOCKS = T // BLOCK
-SCALAR_BLOCKS = 4
+ROUND_SPLIT = 4
+WEAVE_SPLIT = 4
+SCALAR_QUARTERS = [(2, 0), (1, 0), (1, 1)]
+KEEP = 1.0 - LR * WD
 
 
 def weave_words(copy, woven, pairs):
     copy(
-        out=woven.rearrange("p c l -> p (c l)").bitcast(F32).rearrange("p (k c h) -> p k c h", c=BLOCK, h=2),
-        in_=pairs.rearrange("p k h c e -> p k h (c e)").bitcast(F32).rearrange("p k h c -> p k c h"),
+        out=woven.rearrange("p c l -> p (c l)").bitcast(F32).rearrange("p (c u) -> p c u", u=2),
+        in_=pairs.rearrange("p u c e -> p u (c e)").bitcast(F32).rearrange("p u c -> p c u"),
     )
 
 
@@ -75,10 +78,10 @@ def tile_attend_ghub_pl_sgd_kernel(tc, xT, wT, y, wt, xm, offs, out_0, out_1, ou
 
         halves = [slice(0, H), slice(H, N)]
         w16 = [pool.tile([P, H, LANES], BF16, name="w16_%d" % h, align_bytes=64) for h in range(2)]
-        keep = 1.0 - LR * WD
         picked_pairs = [pool.tile([P, 2, N], F32, name="picked%d" % u) for u in range(2)]
         picked = [picked_pairs[t // 2][:, t % 2, :] for t in range(LANES)]
-        decayed = {t: pool.tile([P, H], F32, name="decayed%d" % t) for t in (0, LAST)}
+        vector_half = {0: 1, LAST: 0}
+        decayed = {t: pool.tile([P, H], F32, name="decayed%d" % t) for t in vector_half}
 
         def round_shared(t, sources):
             for h in range(2):
@@ -94,22 +97,25 @@ def tile_attend_ghub_pl_sgd_kernel(tc, xT, wT, y, wt, xm, offs, out_0, out_1, ou
             columns = slice(lo * T // 4, hi * T // 4)
             copy(out=table[t][:, columns], in_=source[t][:, columns])
 
-        for t, scalar_quarters in enumerate([2, 1, 2]):
-            copy_table(scalar_move, t, 0, min(scalar_quarters, 2 - t // 2))
+        def listed(h):
+            return offsets[:, h * H // 16 : (h + 1) * H // 16]
+
+        for t, (ahead, behind) in enumerate(SCALAR_QUARTERS):
+            copy_table(scalar_move, t, 0, ahead)
             nc.vector.tensor_copy(picked[t], source[t][:].indirect(offsets[:]))
             if t < 2:
                 for h in range(2):
                     nc.scalar.copy(out=w16[h][:, :, t], in_=picked[t][:, halves[h]])
-                if t == 0:
-                    nc.vector.tensor_scalar(decayed[t][:], picked[t][:, halves[1]], keep, None, ALU.mult)
             else:
                 round_shared(t, [picked[t][:, half] for half in halves])
-                copy_table(scalar_move, t, 1, 2)
-            copy_table(nc.vector.tensor_copy, t, scalar_quarters, 4)
+            if t in vector_half:
+                nc.vector.tensor_scalar(decayed[t][:], picked[t][:, halves[vector_half[t]]], KEEP, None, ALU.mult)
+            if behind:
+                copy_table(scalar_move, t, ahead, ahead + behind)
+            copy_table(nc.vector.tensor_copy, t, ahead + behind, 4)
         picked_halves = [picked[LAST][:, half] for half in halves]
         for h in range(2):
-            listed = offsets[:, h * H // 16 : (h + 1) * H // 16]
-            nc.vector.tensor_copy(picked_halves[h], source[LAST][:].indirect(listed))
+            nc.vector.tensor_copy(picked_halves[h], source[LAST][:].indirect(listed(h)))
         round_shared(LAST, picked_halves)
 
         w_codes = [pool.tile([P, H], U32, name="w_codes0", align_bytes=64)]
@@ -171,7 +177,8 @@ def tile_attend_ghub_pl_sgd_kernel(tc, xT, wT, y, wt, xm, offs, out_0, out_1, ou
                 for t in range(2 * u, 2 * u + 2):
                     weigh_targets(h, t)
 
-        nc.scalar.activation(decayed[LAST][:], picked_halves[0], COPY, scale=keep)
+        nc.scalar.activation(decayed[LAST][:], picked_halves[vector_half[LAST]], COPY, scale=KEEP)
+
         shared = pool.tile([P, 4 * H], BF16, name="shared", align_bytes=64)
         xm16 = [shared[:], pool.tile([P, 4 * H], BF16, name="xm16_1", align_bytes=64)[:]]
 
@@ -183,7 +190,7 @@ def tile_attend_ghub_pl_sgd_kernel(tc, xT, wT, y, wt, xm, offs, out_0, out_1, ou
 
         g_rows = [
             pool.tile([P, LANES, H], BF16, name="g_rows0"),
-            shared[:, 0 : 4 * H].rearrange("p (t c) -> p t c", t=LANES),
+            shared[:].rearrange("p (t c) -> p t c", t=LANES),
         ]
         pieces = [(0, H), (H, H + H // 2), (H + H // 2, N)]
         g16 = []
@@ -217,8 +224,7 @@ def tile_attend_ghub_pl_sgd_kernel(tc, xT, wT, y, wt, xm, offs, out_0, out_1, ou
         def weave_g(k):
             lo, hi = pieces[k]
             h = lo // H
-            name = "g16_%d" % k
-            g16.append(pool.tile([P, hi - lo, LANES], BF16, name=name, align_bytes=64))
+            g16.append(pool.tile([P, hi - lo, LANES], BF16, name="g16_%d" % k, align_bytes=64))
             nc.vector.tensor_copy(
                 out=g16[k][:].rearrange("p (c i) t -> p c t i", i=4),
                 in_=g_rows[h][:, :, lo - h * H : hi - h * H].rearrange("p t (c i) -> p c t i", i=4),
@@ -245,32 +251,33 @@ def tile_attend_ghub_pl_sgd_kernel(tc, xT, wT, y, wt, xm, offs, out_0, out_1, ou
 
         fresh = {}
 
-        def update(t, first, count, bank_number, on_vector=False):
-            slots = slice(first * H, (first + count) * H)
-            bank = psum.tile([P, count * H], F32, name="bank%d" % bank_number)
+        def update(t, h):
+            bank = psum.tile([P, H], F32, name="bank%d" % (LANES * h + t))
             nc.tensor.matmul_mx(
                 out=bank[:],
                 lhsT=xm_codes[t].bitcast(E4M3),
                 lhsT_scale=xm_scales[t],
-                rhs=g_codes[:, slots].bitcast(E5M2),
-                rhs_scale=g_scales[:, slots],
+                rhs=g_codes[:, halves[h]].bitcast(E5M2),
+                rhs_scale=g_scales[:, halves[h]],
                 start=True,
                 stop=True,
             )
-            values = pool.tile([P, count * H], F32, name="fresh%d_%d" % (t, first))
-            if on_vector:
-                nc.vector.scalar_tensor_tensor(values[:], bank[:], -LR, decayed[t][:], ALU.mult, ALU.add)
+            fresh[t, h] = pool.tile([P, H], F32, name="fresh%d_%d" % (t, h))
+            if vector_half.get(t) == h:
+                rate, old = LR, decayed[t][:]
             else:
-                nc.vector.scalar_tensor_tensor(values[:], bank[:], -LR / keep, picked[t][:, slots], ALU.mult, ALU.add)
-            for e in range(count):
-                fresh[t, first + e] = values[:, e * H : (e + 1) * H]
+                rate, old = LR / KEEP, picked[t][:, halves[h]]
+            nc.vector.scalar_tensor_tensor(fresh[t, h][:], bank[:], -rate, old, ALU.mult, ALU.add)
 
-        def scatter(t, h, on_vector):
-            window = table[t][:].indirect(offsets[:, h * H // 16 : (h + 1) * H // 16])
-            if on_vector:
-                nc.vector.tensor_copy(window, fresh[t, h])
+        def scatter(t, h):
+            window = table[t][:].indirect(listed(h))
+            if vector_half.get(t) == h:
+                nc.vector.tensor_copy(window, fresh[t, h][:])
             else:
-                nc.scalar.activation(window, fresh[t, h], COPY, scale=keep)
+                nc.scalar.activation(window, fresh[t, h][:], COPY, scale=KEEP)
+
+        def store(t):
+            nc.sync.dma_start(out=out_rows[:, t, :], in_=table[t][:])
 
         subtract_targets(0, 0)
         subtract_targets(0, 1)
@@ -294,23 +301,37 @@ def tile_attend_ghub_pl_sgd_kernel(tc, xT, wT, y, wt, xm, offs, out_0, out_1, ou
         quantize_xm(1, 1)
         clamp(1, 0)
         clamp(1, 1)
-        update(0, 0, 1, 0)
-        scatter(0, 0, False)
+        update(0, 0)
+        scatter(0, 0)
         clamp(1, 2)
         for lo, hi in pieces[1:]:
             clamp(1, LAST, lo - H, hi - H)
         weave_g(1)
-        update(1, 0, 1, 1)
-        scatter(1, 0, False)
+        update(1, 0)
+        scatter(1, 0)
         weave_g(2)
         quantize_g(1)
         quantize_xm(2, 2)
         quantize_g(2)
-        update(2, 0, 1, 2)
-        scatter(2, 0, False)
-        update(0, 1, 1, 4, True)
-        update(1, 1, 1, 5)
+        update(2, 0)
+        scatter(2, 0)
+        update(0, 1)
+        update(1, 1)
 
+        scatter(0, 1)
+        store(0)
+        scatter(1, 1)
+        store(1)
+        update(3, 0)
+        update(2, 1)
+        update(3, 1)
+        scatter(3, 0)
+        scatter(2, 1)
+        store(2)
+        scatter(3, 1)
+        store(3)
+
+        pairs = pool.tile([P, BLOCKS, 2, BLOCK, 2], BF16, name="picked1")
 
         def round_pairs(copy, t, lo, hi):
             copy(
@@ -318,33 +339,15 @@ def tile_attend_ghub_pl_sgd_kernel(tc, xT, wT, y, wt, xm, offs, out_0, out_1, ou
                 in_=table[t][:, lo * BLOCK : hi * BLOCK].rearrange("p (k c) -> p k c", c=BLOCK),
             )
 
-        def store(t):
-            nc.sync.dma_start(out=out_rows[:, t, :], in_=table[t][:])
-
-        scatter(0, 1, True)
-        store(0)
-        scatter(1, 1, False)
-        store(1)
-        update(3, 0, 1, 3, True)
-        update(2, 1, 1, 6)
-        update(3, 1, 1, 7)
-        scatter(3, 0, True)
-        scatter(2, 1, False)
-        store(2)
-        scatter(3, 1, False)
-        store(3)
-        split = BLOCKS - SCALAR_BLOCKS
-        pairs = pool.tile([P, BLOCKS, 2, BLOCK, 2], BF16, name="picked1")
         round_pairs(nc.vector.tensor_copy, 0, 0, BLOCKS)
         round_pairs(nc.vector.tensor_copy, 1, 0, BLOCKS)
-        round_pairs(nc.vector.tensor_copy, 2, 0, split)
+        round_pairs(nc.vector.tensor_copy, 2, 0, ROUND_SPLIT)
 
         out_scales = pool.tile([P, T // 4], U8, name="out_scales", align_bytes=64)
         woven = [pool.tile([P, BLOCK, LANES], BF16, name="woven%d" % k, align_bytes=64) for k in range(BLOCKS)]
-        woven_block = [w[:] for w in woven]
 
         def weave(copy, k):
-            weave_words(copy, woven[k][:], pairs[:, k : k + 1])
+            weave_words(copy, woven[k][:], pairs[:, k])
 
         codes = pool.tile([P, T], U32, name="out_codes", align_bytes=64)
 
@@ -353,27 +356,29 @@ def tile_attend_ghub_pl_sgd_kernel(tc, xT, wT, y, wt, xm, offs, out_0, out_1, ou
             nc.vector.quantize_mx(
                 out=codes[:, k * BLOCK : (k + 1) * BLOCK].bitcast(E4M3),
                 scales=out_scales[4 * (k // 2) : P, here],
-                in_=woven_block[k].rearrange("p c l -> p (c l)"),
+                in_=woven[k][:].rearrange("p c l -> p (c l)"),
             )
 
         def store_words(lo, hi):
             columns = slice(lo * BLOCK, hi * BLOCK)
             nc.sync.dma_start(out=words_out[:, columns], in_=codes[:, columns].bitcast(I32))
 
-        for k in range(split, BLOCKS):
+        for k in range(ROUND_SPLIT, BLOCKS):
             round_pairs(nc.scalar.copy, 2, k, k + 1)
-            round_pairs(nc.scalar.copy, 3, k, k + 1)
-            weave(nc.scalar.copy, k)
-        round_pairs(nc.vector.tensor_copy, 3, 0, 2)
-        round_pairs(nc.vector.tensor_copy, 3, 2, split)
-        weave(nc.vector.tensor_copy, 0)
-        weave(nc.vector.tensor_copy, 1)
-        weave(nc.vector.tensor_copy, 2)
+            round_pairs(nc.scalar.copy, LAST, k, k + 1)
+            if k >= WEAVE_SPLIT:
+                weave(nc.scalar.copy, k)
+        round_pairs(nc.vector.tensor_copy, LAST, 0, ROUND_SPLIT // 2)
+        round_pairs(nc.vector.tensor_copy, LAST, ROUND_SPLIT // 2, ROUND_SPLIT)
+        for k in range(3):
+            weave(nc.vector.tensor_copy, k)
         quantize_out(0)
         quantize_out(1)
-        weave(nc.vector.tensor_copy, 3)
-        for lo, hi in [(0, 4), (4, 7), (7, 8)]:
-            for k in range(max(lo, 2), hi):
+        store_words(0, 2)
+        for k in range(3, WEAVE_SPLIT):
+            weave(nc.vector.tensor_copy, k)
+        for lo, hi in [(2, 5), (5, BLOCKS - 1), (BLOCKS - 1, BLOCKS)]:
+            for k in range(lo, hi):
                 quantize_out(k)
             store_words(lo, hi)
         for q in range(4):

@@ -190,10 +190,12 @@ def tile_attend_ghub_pl_sgd_kernel(tc, xT, wT, y, wt, xm, offs, out_0, out_1, ou
 
         g_rows = [
             pool.tile([P, LANES, H], BF16, name="g_rows0"),
-            shared[:].rearrange("p (t c) -> p t c", t=LANES),
+            pool.tile([P, LANES, H], BF16, name="g_rows1"),
         ]
         pieces = [(0, H), (H, H + H // 2), (H + H // 2, N)]
-        g16 = []
+        g16 = [pool.tile([P, H, LANES], BF16, name="g16_0", align_bytes=64)[:]] + [
+            shared[:, e * PASS : (e + 1) * PASS].rearrange("p (c t) -> p c t", t=LANES) for e in range(2)
+        ]
         residual = [
             [pool.tile([P, H], F32, name="residual%d_%d" % (h, t), align_bytes=64) for t in range(LANES)]
             for h in range(2)
@@ -224,9 +226,8 @@ def tile_attend_ghub_pl_sgd_kernel(tc, xT, wT, y, wt, xm, offs, out_0, out_1, ou
         def weave_g(k):
             lo, hi = pieces[k]
             h = lo // H
-            g16.append(pool.tile([P, hi - lo, LANES], BF16, name="g16_%d" % k, align_bytes=64))
             nc.vector.tensor_copy(
-                out=g16[k][:].rearrange("p (c i) t -> p c t i", i=4),
+                out=g16[k].rearrange("p (c i) t -> p c t i", i=4),
                 in_=g_rows[h][:, :, lo - h * H : hi - h * H].rearrange("p t (c i) -> p c t i", i=4),
             )
 
@@ -235,7 +236,7 @@ def tile_attend_ghub_pl_sgd_kernel(tc, xT, wT, y, wt, xm, offs, out_0, out_1, ou
             nc.vector.quantize_mx(
                 out=g_codes[:, lo:hi].bitcast(E5M2),
                 scales=g_scales[:, lo:hi],
-                in_=g16[k][:].rearrange("p i t -> p (i t)"),
+                in_=g16[k].rearrange("p i t -> p (i t)"),
             )
 
         def quantize_xm(first, count):
@@ -297,22 +298,19 @@ def tile_attend_ghub_pl_sgd_kernel(tc, xT, wT, y, wt, xm, offs, out_0, out_1, ou
         subtract_targets(1, 2)
         quantize_g(0)
         subtract_targets(1, 3)
+        for t in range(LANES):
+            clamp(1, t)
         quantize_xm(0, 1)
         quantize_xm(1, 1)
-        clamp(1, 0)
-        clamp(1, 1)
+        weave_g(1)
+        weave_g(2)
         update(0, 0)
         scatter(0, 0)
-        clamp(1, 2)
-        for lo, hi in pieces[1:]:
-            clamp(1, LAST, lo - H, hi - H)
-        weave_g(1)
-        update(1, 0)
-        scatter(1, 0)
-        weave_g(2)
         quantize_g(1)
         quantize_xm(2, 2)
         quantize_g(2)
+        update(1, 0)
+        scatter(1, 0)
         update(2, 0)
         scatter(2, 0)
         update(0, 1)

@@ -80,8 +80,9 @@ def tile_attend_ghub_pl_sgd_kernel(tc, xT, wT, y, wt, xm, offs, out_0, out_1, ou
         w16 = [pool.tile([P, H, LANES], BF16, name="w16_%d" % h, align_bytes=64) for h in range(2)]
         picked_pairs = [pool.tile([P, 2, N], F32, name="picked%d" % u) for u in range(2)]
         picked = [picked_pairs[t // 2][:, t % 2, :] for t in range(LANES)]
-        vector_half = {0: 1, LAST: 0}
+        vector_half = {0: 1}
         decayed = {t: pool.tile([P, H], F32, name="decayed%d" % t) for t in vector_half}
+        decayed_last = pool.tile([P, N], F32, name="decayed_last")
 
         def round_shared(t, sources):
             for h in range(2):
@@ -177,7 +178,7 @@ def tile_attend_ghub_pl_sgd_kernel(tc, xT, wT, y, wt, xm, offs, out_0, out_1, ou
                 for t in range(2 * u, 2 * u + 2):
                     weigh_targets(h, t)
 
-        nc.scalar.activation(decayed[LAST][:], picked_halves[vector_half[LAST]], COPY, scale=KEEP)
+        nc.scalar.activation(decayed_last[:], picked[LAST], COPY, scale=KEEP)
 
         shared = pool.tile([P, 4 * H], BF16, name="shared", align_bytes=64)
         xm16 = [shared[:], pool.tile([P, 4 * H], BF16, name="xm16_1", align_bytes=64)[:]]
@@ -253,7 +254,7 @@ def tile_attend_ghub_pl_sgd_kernel(tc, xT, wT, y, wt, xm, offs, out_0, out_1, ou
         fresh = {}
 
         def update(t, h):
-            bank = psum.tile([P, H], F32, name="bank%d" % (LANES * h + t))
+            bank = psum.tile([P, H], F32, name="bank%d" % (LANES if (t, h) == (2, 0) else LANES * h + t))
             nc.tensor.matmul_mx(
                 out=bank[:],
                 lhsT=xm_codes[t].bitcast(E4M3),
@@ -311,8 +312,6 @@ def tile_attend_ghub_pl_sgd_kernel(tc, xT, wT, y, wt, xm, offs, out_0, out_1, ou
         quantize_g(2)
         update(1, 0)
         scatter(1, 0)
-        update(2, 0)
-        scatter(2, 0)
         update(0, 1)
         update(1, 1)
 
@@ -320,32 +319,51 @@ def tile_attend_ghub_pl_sgd_kernel(tc, xT, wT, y, wt, xm, offs, out_0, out_1, ou
         store(0)
         scatter(1, 1)
         store(1)
-        update(3, 0)
+        update(2, 0)
+        scatter(2, 0)
+        bank = psum.tile([P, N], F32, name="bank3")
+        nc.tensor.matmul_mx(
+            out=bank[:],
+            lhsT=xm_codes[LAST].bitcast(E4M3),
+            lhsT_scale=xm_scales[LAST],
+            rhs=g_codes[:].bitcast(E5M2),
+            rhs_scale=g_scales[:],
+            start=True,
+            stop=True,
+        )
+        nc.vector.scalar_tensor_tensor(picked[LAST], bank[:], -LR, decayed_last[:], ALU.mult, ALU.add)
         update(2, 1)
-        update(3, 1)
-        scatter(3, 0)
+        nc.vector.tensor_copy(table[LAST][:].indirect(offsets[:]), picked[LAST])
+        store(LAST)
         scatter(2, 1)
         store(2)
-        scatter(3, 1)
-        store(3)
 
-        pairs = pool.tile([P, BLOCKS, 2, BLOCK, 2], BF16, name="picked1")
+        SHARE = BLOCKS // 2
+        pairs = [
+            pool.tile([P, SHARE, 2, BLOCK, 2], BF16, name=name) for name in ("pairs0", "picked1")
+        ]
 
         def round_pairs(copy, t, lo, hi):
+            first = lo // SHARE * SHARE
             copy(
-                out=pairs[:, lo:hi, t // 2, :, t % 2],
+                out=pairs[lo // SHARE][:, lo - first : hi - first, t // 2, :, t % 2],
                 in_=table[t][:, lo * BLOCK : hi * BLOCK].rearrange("p (k c) -> p k c", c=BLOCK),
             )
 
-        round_pairs(nc.vector.tensor_copy, 0, 0, BLOCKS)
-        round_pairs(nc.vector.tensor_copy, 1, 0, BLOCKS)
-        round_pairs(nc.vector.tensor_copy, 2, 0, ROUND_SPLIT)
+        def gpsimd_round(out, in_):
+            nc.gpsimd.tensor_scalar(out, in_, 1.0, 1.0, ALU.mult, ALU.mult)
+
+        for t in range(2):
+            round_pairs(gpsimd_round, t, 0, SHARE)
+        for t in range(2):
+            round_pairs(nc.vector.tensor_copy, t, SHARE, BLOCKS)
+        round_pairs(nc.vector.tensor_copy, LAST, 0, ROUND_SPLIT)
 
         out_scales = pool.tile([P, T // 4], U8, name="out_scales", align_bytes=64)
         woven = [pool.tile([P, BLOCK, LANES], BF16, name="woven%d" % k, align_bytes=64) for k in range(BLOCKS)]
 
         def weave(copy, k):
-            weave_words(copy, woven[k][:], pairs[:, k])
+            weave_words(copy, woven[k][:], pairs[k // SHARE][:, k % SHARE])
 
         codes = pool.tile([P, T], U32, name="out_codes", align_bytes=64)
 
@@ -362,12 +380,12 @@ def tile_attend_ghub_pl_sgd_kernel(tc, xT, wT, y, wt, xm, offs, out_0, out_1, ou
             nc.sync.dma_start(out=words_out[:, columns], in_=codes[:, columns].bitcast(I32))
 
         for k in range(ROUND_SPLIT, BLOCKS):
-            round_pairs(nc.scalar.copy, 2, k, k + 1)
             round_pairs(nc.scalar.copy, LAST, k, k + 1)
+            round_pairs(nc.scalar.copy, 2, k, k + 1)
             if k >= WEAVE_SPLIT:
                 weave(nc.scalar.copy, k)
-        round_pairs(nc.vector.tensor_copy, LAST, 0, ROUND_SPLIT // 2)
-        round_pairs(nc.vector.tensor_copy, LAST, ROUND_SPLIT // 2, ROUND_SPLIT)
+        round_pairs(nc.vector.tensor_copy, 2, 0, ROUND_SPLIT // 2)
+        round_pairs(nc.vector.tensor_copy, 2, ROUND_SPLIT // 2, ROUND_SPLIT)
         for k in range(3):
             weave(nc.vector.tensor_copy, k)
         quantize_out(0)
@@ -375,7 +393,7 @@ def tile_attend_ghub_pl_sgd_kernel(tc, xT, wT, y, wt, xm, offs, out_0, out_1, ou
         store_words(0, 2)
         for k in range(3, WEAVE_SPLIT):
             weave(nc.vector.tensor_copy, k)
-        for lo, hi in [(2, 5), (5, BLOCKS - 1), (BLOCKS - 1, BLOCKS)]:
+        for lo, hi in [(2, 4), (4, 6), (6, BLOCKS)]:
             for k in range(lo, hi):
                 quantize_out(k)
             store_words(lo, hi)

@@ -80,9 +80,8 @@ def tile_attend_ghub_pl_sgd_kernel(tc, xT, wT, y, wt, xm, offs, out_0, out_1, ou
         w16 = [pool.tile([P, H, LANES], BF16, name="w16_%d" % h, align_bytes=64) for h in range(2)]
         picked_pairs = [pool.tile([P, 2, N], F32, name="picked%d" % u) for u in range(2)]
         picked = [picked_pairs[t // 2][:, t % 2, :] for t in range(LANES)]
-        vector_half = {0: 1}
+        vector_half = {0: 1, 1: 1, 2: 1}
         decayed = {t: pool.tile([P, H], F32, name="decayed%d" % t) for t in vector_half}
-        decayed_last = pool.tile([P, N], F32, name="decayed_last")
 
         def round_shared(t, sources):
             for h in range(2):
@@ -178,8 +177,6 @@ def tile_attend_ghub_pl_sgd_kernel(tc, xT, wT, y, wt, xm, offs, out_0, out_1, ou
                 for t in range(2 * u, 2 * u + 2):
                     weigh_targets(h, t)
 
-        nc.scalar.activation(decayed_last[:], picked[LAST], COPY, scale=KEEP)
-
         shared = pool.tile([P, 4 * H], BF16, name="shared", align_bytes=64)
         xm16 = [shared[:], pool.tile([P, 4 * H], BF16, name="xm16_1", align_bytes=64)[:]]
 
@@ -254,7 +251,7 @@ def tile_attend_ghub_pl_sgd_kernel(tc, xT, wT, y, wt, xm, offs, out_0, out_1, ou
         fresh = {}
 
         def update(t, h):
-            bank = psum.tile([P, H], F32, name="bank%d" % (LANES if (t, h) == (2, 0) else LANES * h + t))
+            bank = psum.tile([P, H], F32, name="bank%d" % (LANES * h + t))
             nc.tensor.matmul_mx(
                 out=bank[:],
                 lhsT=xm_codes[t].bitcast(E4M3),
@@ -312,31 +309,23 @@ def tile_attend_ghub_pl_sgd_kernel(tc, xT, wT, y, wt, xm, offs, out_0, out_1, ou
         quantize_g(2)
         update(1, 0)
         scatter(1, 0)
+        update(2, 0)
+        scatter(2, 0)
         update(0, 1)
         update(1, 1)
 
         scatter(0, 1)
         store(0)
+        update(3, 0)
+        scatter(3, 0)
+        update(2, 1)
         scatter(1, 1)
         store(1)
-        update(2, 0)
-        scatter(2, 0)
-        bank = psum.tile([P, N], F32, name="bank3")
-        nc.tensor.matmul_mx(
-            out=bank[:],
-            lhsT=xm_codes[LAST].bitcast(E4M3),
-            lhsT_scale=xm_scales[LAST],
-            rhs=g_codes[:].bitcast(E5M2),
-            rhs_scale=g_scales[:],
-            start=True,
-            stop=True,
-        )
-        nc.vector.scalar_tensor_tensor(picked[LAST], bank[:], -LR, decayed_last[:], ALU.mult, ALU.add)
-        update(2, 1)
-        nc.vector.tensor_copy(table[LAST][:].indirect(offsets[:]), picked[LAST])
-        store(LAST)
+        update(3, 1)
         scatter(2, 1)
         store(2)
+        scatter(3, 1)
+        store(3)
 
         SHARE = BLOCKS // 2
         pairs = [
@@ -357,7 +346,7 @@ def tile_attend_ghub_pl_sgd_kernel(tc, xT, wT, y, wt, xm, offs, out_0, out_1, ou
             round_pairs(gpsimd_round, t, 0, SHARE)
         for t in range(2):
             round_pairs(nc.vector.tensor_copy, t, SHARE, BLOCKS)
-        round_pairs(nc.vector.tensor_copy, LAST, 0, ROUND_SPLIT)
+        round_pairs(nc.vector.tensor_copy, 2, 0, ROUND_SPLIT)
 
         out_scales = pool.tile([P, T // 4], U8, name="out_scales", align_bytes=64)
         woven = [pool.tile([P, BLOCK, LANES], BF16, name="woven%d" % k, align_bytes=64) for k in range(BLOCKS)]
@@ -380,12 +369,12 @@ def tile_attend_ghub_pl_sgd_kernel(tc, xT, wT, y, wt, xm, offs, out_0, out_1, ou
             nc.sync.dma_start(out=words_out[:, columns], in_=codes[:, columns].bitcast(I32))
 
         for k in range(ROUND_SPLIT, BLOCKS):
-            round_pairs(nc.scalar.copy, LAST, k, k + 1)
             round_pairs(nc.scalar.copy, 2, k, k + 1)
+            round_pairs(nc.scalar.copy, LAST, k, k + 1)
             if k >= WEAVE_SPLIT:
                 weave(nc.scalar.copy, k)
-        round_pairs(nc.vector.tensor_copy, 2, 0, ROUND_SPLIT // 2)
-        round_pairs(nc.vector.tensor_copy, 2, ROUND_SPLIT // 2, ROUND_SPLIT)
+        round_pairs(nc.vector.tensor_copy, LAST, 0, ROUND_SPLIT // 2)
+        round_pairs(nc.vector.tensor_copy, LAST, ROUND_SPLIT // 2, ROUND_SPLIT)
         for k in range(3):
             weave(nc.vector.tensor_copy, k)
         quantize_out(0)

@@ -27,6 +27,7 @@ BLOCKS = T // BLOCK
 ROUND_SPLIT = 4
 WEAVE_SPLIT = 4
 SCALAR_QUARTERS = [(2, 0), (1, 0), (1, 1)]
+GPSIMD_BLOCKS = 3
 KEEP = 1.0 - LR * WD
 
 
@@ -327,32 +328,33 @@ def tile_attend_ghub_pl_sgd_kernel(tc, xT, wT, y, wt, xm, offs, out_0, out_1, ou
         scatter(3, 1)
         store(3)
 
-        SHARE = BLOCKS // 2
+        counts = (BLOCKS - GPSIMD_BLOCKS, GPSIMD_BLOCKS)
         pairs = [
-            pool.tile([P, SHARE, 2, BLOCK, 2], BF16, name=name) for name in ("pairs0", "picked1")
+            pool.tile([P, 2, count * BLOCK, 2], BF16, name=name) for count, name in zip(counts, ("picked1", "pairs1"))
         ]
 
+        def paired(lo, hi):
+            part = lo // counts[0]
+            first = part * counts[0]
+            return pairs[part][:, :, (lo - first) * BLOCK : (hi - first) * BLOCK, :]
+
         def round_pairs(copy, t, lo, hi):
-            first = lo // SHARE * SHARE
-            copy(
-                out=pairs[lo // SHARE][:, lo - first : hi - first, t // 2, :, t % 2],
-                in_=table[t][:, lo * BLOCK : hi * BLOCK].rearrange("p (k c) -> p k c", c=BLOCK),
-            )
+            copy(out=paired(lo, hi)[:, t // 2, :, t % 2], in_=table[t][:, lo * BLOCK : hi * BLOCK])
 
         def gpsimd_round(out, in_):
             nc.gpsimd.tensor_scalar(out, in_, 1.0, 1.0, ALU.mult, ALU.mult)
 
         for t in range(2):
-            round_pairs(gpsimd_round, t, 0, SHARE)
+            round_pairs(gpsimd_round, t, counts[0], BLOCKS)
         for t in range(2):
-            round_pairs(nc.vector.tensor_copy, t, SHARE, BLOCKS)
+            round_pairs(nc.vector.tensor_copy, t, 0, counts[0])
         round_pairs(nc.vector.tensor_copy, 2, 0, ROUND_SPLIT)
 
         out_scales = pool.tile([P, T // 4], U8, name="out_scales", align_bytes=64)
         woven = [pool.tile([P, BLOCK, LANES], BF16, name="woven%d" % k, align_bytes=64) for k in range(BLOCKS)]
 
         def weave(copy, k):
-            weave_words(copy, woven[k][:], pairs[k // SHARE][:, k % SHARE])
+            weave_words(copy, woven[k][:], paired(k, k + 1))
 
         codes = pool.tile([P, T], U32, name="out_codes", align_bytes=64)
 

from contextlib import ExitStack

import concourse.mybir as mybir

D, T, N, R = 512, 2048, 512, 512
LR, WD = 0.1, 0.5
FLOPS = 2 * 2 * R * D * N

F32 = mybir.dt.float32
BF16 = mybir.dt.bfloat16
I32 = mybir.dt.int32
U32 = mybir.dt.uint32
U16 = mybir.dt.uint16
U8 = mybir.dt.uint8
E4M3 = mybir.dt.float8_e4m3fn_x4
E5M2 = mybir.dt.float8_e5m2_x4
ALU = mybir.AluOpType
COPY = mybir.ActivationFunctionType.Copy

P = 128
LANES = 4
LAST = LANES - 1
H = N // 2
PASS = P * LANES
BLOCK = 256
BLOCKS = T // BLOCK
ROUND_SPLIT = 4
WEAVE_SPLIT = 4
SCALAR_QUARTERS = [(2, 0), (1, 0), (1, 1)]
GPSIMD_BLOCKS = 3
KEEP = 1.0 - LR * WD


def weave_words(copy, woven, pairs):
    copy(
        out=woven.rearrange("p c l -> p (c l)").bitcast(F32).rearrange("p (c u) -> p c u", u=2),
        in_=pairs.rearrange("p u c e -> p u (c e)").bitcast(F32).rearrange("p u c -> p c u"),
    )


def tile_attend_ghub_pl_sgd_kernel(tc, xT, wT, y, wt, xm, offs, out_0, out_1, out_2):
    nc = tc.nc
    w_rows = wT.rearrange("(p t) c -> p t c", t=LANES)
    out_rows = out_0.rearrange("(p t) c -> p t c", t=LANES)
    x_rows = xT[0].rearrange("(p j) r -> p j r", j=LANES)
    xm_rows = xm[0].rearrange("(p j) d -> p j d", j=LANES)
    y_rows = y[0].rearrange("(p t) i -> p t i", t=LANES)
    wt_rows = wt[0].rearrange("(p t) o -> p (t o)", t=LANES)
    words_out = out_1[0].rearrange("p c l -> p (c l)").bitcast(I32)
    scales_out = out_2[0].bitcast(I32)

    with ExitStack() as ctx:
        pool = ctx.enter_context(tc.tile_pool(name="pool", bufs=1))
        psum = ctx.enter_context(tc.psum_pool(name="psum", bufs=1))

        offsets = pool.tile([P, N // 16], U16, name="offsets")
        source = [pool.tile([P, T], F32, name="source%d" % t) for t in range(LANES)]
        table = [pool.tile([P, T], F32, name="table%d" % t) for t in range(LANES)]
        x_raw = pool.tile([P, LANES, R], F32, name="x_raw")
        xm_raw = pool.tile([P, LANES, D], F32, name="xm_raw", align_bytes=64)
        y_pairs = [pool.tile([P, 2, N], F32, name="y_pair%d" % u) for u in range(2)]
        y_raw = [y_pairs[t // 2][:, t % 2, :] for t in range(LANES)]
        weights = pool.tile([P, LANES], F32, name="weights")
        weight = [weights[:, t : t + 1] for t in range(LANES)]

        nc.sync.dma_start(out=source[0][:], in_=w_rows[:, 0, :])
        nc.sync.dma_start(offsets[:], offs)
        for t in range(1, LANES):
            nc.sync.dma_start(out=source[t][:], in_=w_rows[:, t, :])
        nc.sync.dma_start(out=x_raw[:], in_=x_rows)
        nc.sync.dma_start(out=weights[:], in_=wt_rows)
        for u in range(2):
            nc.sync.dma_start(out=y_pairs[u][:], in_=y_rows[:, 2 * u : 2 * u + 2, :])
        nc.sync.dma_start(out=xm_raw[:], in_=xm_rows)
        nc.sync.dma_start(out=table[LAST][:], in_=w_rows[:, LAST, :])

        g_codes = pool.tile([P, N], U32, name="g_codes", align_bytes=64)
        g_scales = pool.tile([P, N], U8, name="g_scales", align_bytes=64)

        halves = [slice(0, H), slice(H, N)]
        w16 = [pool.tile([P, H, LANES], BF16, name="w16_%d" % h, align_bytes=64) for h in range(2)]
        picked_pairs = [pool.tile([P, 2, N], F32, name="picked%d" % u) for u in range(2)]
        picked = [picked_pairs[t // 2][:, t % 2, :] for t in range(LANES)]
        vector_half = {0: 1, 1: 1, 2: 1}
        decayed = {t: pool.tile([P, H], F32, name="decayed%d" % t) for t in vector_half}

        def round_shared(t, sources):
            for h in range(2):
                for q in range(2):
                    copy = nc.scalar.copy if h == q else nc.vector.tensor_copy
                    quarter = slice(q * H // 2, (q + 1) * H // 2)
                    copy(out=w16[h][:, quarter, t], in_=sources[h][:, quarter])

        def scalar_move(out, in_):
            nc.scalar.activation(out, in_, COPY)

        def copy_table(copy, t, lo, hi):
            columns = slice(lo * T // 4, hi * T // 4)
            copy(out=table[t][:, columns], in_=source[t][:, columns])

        def listed(h):
            return offsets[:, h * H // 16 : (h + 1) * H // 16]

        for t, (ahead, behind) in enumerate(SCALAR_QUARTERS):
            copy_table(scalar_move, t, 0, ahead)
            nc.vector.tensor_copy(picked[t], source[t][:].indirect(offsets[:]))
            if t < 2:
                for h in range(2):
                    nc.scalar.copy(out=w16[h][:, :, t], in_=picked[t][:, halves[h]])
            else:
                round_shared(t, [picked[t][:, half] for half in halves])
            if t in vector_half:
                nc.vector.tensor_scalar(decayed[t][:], picked[t][:, halves[vector_half[t]]], KEEP, None, ALU.mult)
            if behind:
                copy_table(scalar_move, t, ahead, ahead + behind)
            copy_table(nc.vector.tensor_copy, t, ahead + behind, 4)
        picked_halves = [picked[LAST][:, half] for half in halves]
        for h in range(2):
            nc.vector.tensor_copy(picked_halves[h], source[LAST][:].indirect(listed(h)))
        round_shared(LAST, picked_halves)

        w_codes = [pool.tile([P, H], U32, name="w_codes0", align_bytes=64)]
        w_scales = [pool.tile([P, H], U8, name="w_scales%d" % h, align_bytes=64) for h in range(2)]

        def quantize_w(h):
            nc.vector.quantize_mx(
                out=w_codes[h][:].bitcast(E4M3), scales=w_scales[h][:], in_=w16[h][:].rearrange("p i t -> p (i t)")
            )

        quantize_w(0)

        x16 = [pool.tile([P, 2, P, LANES], BF16, name="x16_%d" % u, align_bytes=64) for u in range(2)]
        x_by_pair = x_raw[:].rearrange("p j (s u e) -> p u s j e", u=2, e=2)
        x_codes = [pool.tile([P, P], U32, name="x_codes%d" % t, align_bytes=64) for t in range(LANES)]
        x_scales = [pool.tile([P, P], U8, name="x_scales%d" % t, align_bytes=64) for t in range(LANES)]
        scores = [
            [psum.tile([P, H], F32, name="bank%d" % (LANES * h + t)) for t in range(LANES)] for h in range(2)
        ]
        weighted_y = [pool.tile([P, LANES, H], F32, name="weighted_y%d" % h) for h in range(2)]

        def deal_x(copy, u):
            copy(out=x16[u][:].rearrange("p e s j -> p s j e"), in_=x_by_pair[:, u])

        def quantize_x(t):
            nc.vector.quantize_mx(
                out=x_codes[t][:].bitcast(E4M3),
                scales=x_scales[t][:],
                in_=x16[t // 2][:, t % 2].rearrange("p s j -> p (s j)"),
            )

        def score(h, t):
            nc.tensor.matmul_mx(
                out=scores[h][t][:],
                lhsT=x_codes[t][:].bitcast(E4M3),
                lhsT_scale=x_scales[t][:],
                rhs=w_codes[h][:].bitcast(E4M3),
                rhs_scale=w_scales[h][:],
                start=True,
                stop=True,
            )

        def weigh_targets(h, t):
            nc.scalar.activation(weighted_y[h][:, t, :], y_raw[t][:, halves[h]], COPY, scale=weight[t])

        deal_x(nc.vector.tensor_copy, 0)
        deal_x(nc.scalar.copy, 1)
        upper = pool.tile([P, LANES], F32, name="upper")
        lower = pool.tile([P, LANES], F32, name="lower")
        nc.vector.scalar_tensor_tensor(upper[:], weights[:], -1.0, weights[:], ALU.mult, ALU.max)
        nc.vector.scalar_tensor_tensor(lower[:], weights[:], -1.0, weights[:], ALU.mult, ALU.min)
        for t in range(2):
            quantize_x(t)
            score(0, t)
        w_codes.append(pool.tile([P, H], U32, name="x16_0", align_bytes=64))
        quantize_w(1)
        for u in range(2):
            for h in range(2):
                for t in range(2 * u, 2 * u + 2):
                    weigh_targets(h, t)

        shared = pool.tile([P, 4 * H], BF16, name="shared", align_bytes=64)
        xm16 = [shared[:], pool.tile([P, 4 * H], BF16, name="xm16_1", align_bytes=64)[:]]

        for u in range(2):
            nc.scalar.copy(
                out=xm16[u].rearrange("p (e s j) -> p s j e", e=2, j=LANES),
                in_=xm_raw[:].rearrange("p j (s u e) -> p u s j e", u=2, e=2)[:, u],
            )

        g_rows = [
            pool.tile([P, LANES, H], BF16, name="g_rows0"),
            pool.tile([P, LANES, H], BF16, name="g_rows1"),
        ]
        pieces = [(0, H), (H, H + H // 2), (H + H // 2, N)]
        g16 = [pool.tile([P, H, LANES], BF16, name="g16_0", align_bytes=64)[:]] + [
            shared[:, e * PASS : (e + 1) * PASS].rearrange("p (c t) -> p c t", t=LANES) for e in range(2)
        ]
        residual = [
            [pool.tile([P, H], F32, name="residual%d_%d" % (h, t), align_bytes=64) for t in range(LANES)]
            for h in range(2)
        ]
        xm_codes = []
        xm_scales = []

        def subtract_targets(h, t):
            nc.vector.scalar_tensor_tensor(
                residual[h][t][:],
                scores[h][t][:],
                weight[t],
                weighted_y[h][:, t, :],
                ALU.mult,
                ALU.subtract,
            )

        def clamp(h, t, lo=0, hi=H):
            nc.vector.tensor_scalar(
                g_rows[h][:, t, lo:hi],
                residual[h][t][:, lo:hi],
                lower[:, t : t + 1],
                upper[:, t : t + 1],
                ALU.max,
                ALU.min,
            )

        def weave_g(k):
            lo, hi = pieces[k]
            h = lo // H
            nc.vector.tensor_copy(
                out=g16[k].rearrange("p (c i) t -> p c t i", i=4),
                in_=g_rows[h][:, :, lo - h * H : hi - h * H].rearrange("p t (c i) -> p c t i", i=4),
            )

        def quantize_g(k):
            lo, hi = pieces[k]
            nc.vector.quantize_mx(
                out=g_codes[:, lo:hi].bitcast(E5M2),
                scales=g_scales[:, lo:hi],
                in_=g16[k].rearrange("p i t -> p (i t)"),
            )

        def quantize_xm(first, count):
            codes = pool.tile([P, count * P], U32, name="xm_codes%d" % first, align_bytes=64)
            scales = pool.tile([P, count * P], U8, name="xm_scales%d" % first, align_bytes=64)
            start = (first % 2) * PASS
            nc.vector.quantize_mx(
                out=codes[:].bitcast(E4M3), scales=scales[:], in_=xm16[first // 2][:, start : start + count * PASS]
            )
            for e in range(count):
                xm_codes.append(codes[:, e * P : (e + 1) * P])
                xm_scales.append(scales[:, e * P : (e + 1) * P])

        fresh = {}

        def update(t, h):
            bank = psum.tile([P, H], F32, name="bank%d" % (LANES * h + t))
            nc.tensor.matmul_mx(
                out=bank[:],
                lhsT=xm_codes[t].bitcast(E4M3),
                lhsT_scale=xm_scales[t],
                rhs=g_codes[:, halves[h]].bitcast(E5M2),
                rhs_scale=g_scales[:, halves[h]],
                start=True,
                stop=True,
            )
            fresh[t, h] = pool.tile([P, H], F32, name="fresh%d_%d" % (t, h))
            if vector_half.get(t) == h:
                rate, old = LR, decayed[t][:]
            else:
                rate, old = LR / KEEP, picked[t][:, halves[h]]
            nc.vector.scalar_tensor_tensor(fresh[t, h][:], bank[:], -rate, old, ALU.mult, ALU.add)

        def scatter(t, h):
            window = table[t][:].indirect(listed(h))
            if vector_half.get(t) == h:
                nc.vector.tensor_copy(window, fresh[t, h][:])
            else:
                nc.scalar.activation(window, fresh[t, h][:], COPY, scale=KEEP)

        def store(t):
            nc.sync.dma_start(out=out_rows[:, t, :], in_=table[t][:])

        subtract_targets(0, 0)
        subtract_targets(0, 1)
        for t in range(2, LANES):
            quantize_x(t)
            score(0, t)
        for t in range(LANES):
            score(1, t)
        clamp(0, 0)
        for t in range(2, LANES):
            subtract_targets(0, t)
            clamp(0, t - 1)
        subtract_targets(1, 0)
        clamp(0, LAST)
        subtract_targets(1, 1)
        weave_g(0)
        subtract_targets(1, 2)
        quantize_g(0)
        subtract_targets(1, 3)
        for t in range(LANES):
            clamp(1, t)
        quantize_xm(0, 1)
        quantize_xm(1, 1)
        weave_g(1)
        weave_g(2)
        update(0, 0)
        scatter(0, 0)
        quantize_g(1)
        quantize_xm(2, 2)
        quantize_g(2)
        update(1, 0)
        scatter(1, 0)
        update(2, 0)
        scatter(2, 0)
        update(0, 1)
        update(1, 1)

        scatter(0, 1)
        store(0)
        update(3, 0)
        scatter(3, 0)
        update(2, 1)
        scatter(1, 1)
        store(1)
        update(3, 1)
        scatter(2, 1)
        store(2)
        scatter(3, 1)
        store(3)

        counts = (BLOCKS - GPSIMD_BLOCKS, GPSIMD_BLOCKS)
        pairs = [
            pool.tile([P, 2, count * BLOCK, 2], BF16, name=name) for count, name in zip(counts, ("picked1", "pairs1"))
        ]

        def paired(lo, hi):
            part = lo // counts[0]
            first = part * counts[0]
            return pairs[part][:, :, (lo - first) * BLOCK : (hi - first) * BLOCK, :]

        def round_pairs(copy, t, lo, hi):
            copy(out=paired(lo, hi)[:, t // 2, :, t % 2], in_=table[t][:, lo * BLOCK : hi * BLOCK])

        def gpsimd_round(out, in_):
            nc.gpsimd.tensor_scalar(out, in_, 1.0, 1.0, ALU.mult, ALU.mult)

        for t in range(2):
            round_pairs(gpsimd_round, t, counts[0], BLOCKS)
        for t in range(2):
            round_pairs(nc.vector.tensor_copy, t, 0, counts[0])
        round_pairs(nc.vector.tensor_copy, 2, 0, ROUND_SPLIT)

        out_scales = pool.tile([P, T // 4], U8, name="out_scales", align_bytes=64)
        woven = [pool.tile([P, BLOCK, LANES], BF16, name="woven%d" % k, align_bytes=64) for k in range(BLOCKS)]

        def weave(copy, k):
            weave_words(copy, woven[k][:], paired(k, k + 1))

        codes = pool.tile([P, T], U32, name="out_codes", align_bytes=64)

        def quantize_out(k):
            here = slice(k % 2 * BLOCK, (k % 2 + 1) * BLOCK)
            nc.vector.quantize_mx(
                out=codes[:, k * BLOCK : (k + 1) * BLOCK].bitcast(E4M3),
                scales=out_scales[4 * (k // 2) : P, here],
                in_=woven[k][:].rearrange("p c l -> p (c l)"),
            )

        def store_words(lo, hi):
            columns = slice(lo * BLOCK, hi * BLOCK)
            nc.sync.dma_start(out=words_out[:, columns], in_=codes[:, columns].bitcast(I32))

        for k in range(ROUND_SPLIT, BLOCKS):
            round_pairs(nc.scalar.copy, 2, k, k + 1)
            round_pairs(nc.scalar.copy, LAST, k, k + 1)
            if k >= WEAVE_SPLIT:
                weave(nc.scalar.copy, k)
        round_pairs(nc.vector.tensor_copy, LAST, 0, ROUND_SPLIT // 2)
        round_pairs(nc.vector.tensor_copy, LAST, ROUND_SPLIT // 2, ROUND_SPLIT)
        for k in range(3):
            weave(nc.vector.tensor_copy, k)
        quantize_out(0)
        quantize_out(1)
        store_words(0, 2)
        for k in range(3, WEAVE_SPLIT):
            weave(nc.vector.tensor_copy, k)
        for lo, hi in [(2, 4), (4, 6), (6, BLOCKS)]:
            for k in range(lo, hi):
                quantize_out(k)
            store_words(lo, hi)
        for q in range(4):
            nc.sync.dma_start(
                out=scales_out[4 * q : 4 * q + 4, :].rearrange("f (g w) -> g f w", g=4),
                in_=out_scales[32 * q : 32 * q + 16, :].bitcast(I32),
            )
